import numpy as np, ml_dtypes
CORES = [5,29,101,125,133,157,229,253]
N = 8
import mx_ref
BF = ml_dtypes.bfloat16
def pick(q, e):
    c = np.concatenate([q[0].reshape(128, -1, 4), np.zeros((128, 1, 4), np.uint8)], axis=1); s = np.concatenate([q[1], np.ones((16, 1), np.uint8)], axis=1)
    return (np.ascontiguousarray(c[:, e].reshape(128, -1)), np.ascontiguousarray(s[:, e]))
def join(*qs):
    return (np.concatenate([q[0] for q in qs], axis=1), np.concatenate([q[1] for q in qs], axis=1))
def put(q, e, v):
    c, s = q[0].reshape(128, -1, 4).copy(), q[1].copy(); c[:, e] = v[0].reshape(128, -1, 4); s[:, e] = v[1]
    return (c.reshape(128, -1), s)
def pk(c, s):
    return (np.ascontiguousarray(c), mx_ref.live(s))
def emit(q):
    return q[0], q[1]
def tile(rs):
    return np.stack(rs, axis=2).reshape(128, -1).astype(BF)
def cut(t, i, w=512):
    return t[:, w * i:w * i + w]
def f(rng, *shape):
    return mx_ref.flush((rng.standard_normal(shape, dtype=np.float32) * np.exp2(rng.integers(-2, 3, shape[:-1] + (1,)))).astype(BF))
def wide(rng, *shape, cols=0):
    v = rng.standard_normal(shape, dtype=np.float32) * np.exp2(rng.integers(-12, 13, shape)).astype(np.float32)
    if cols: v *= np.repeat(np.exp2(rng.integers(-cols, cols + 1, shape[:-2] + (1, shape[-1] // 4))) * (rng.random(shape[:-2] + (1, shape[-1] // 4)) > 0.0625), 4, axis=-1).astype(np.float32)
    return mx_ref.flush(v.astype(BF))
T, CAPP, CAPR = 128, 48, 32
def same(t):
    return np.stack([np.concatenate([t, np.zeros((128, 512 - t.shape[1]), BF)], axis=1)] * N)
def bf(t):
    return np.asarray(t, np.float32).astype(BF)
def sized(rng, *shape):
    return 1 + rng.random(shape)
def signs(rng, *shape):
    return 1 - 2 * rng.integers(0, 2, shape)
def setup_inputs(rng):
    return {"x": f(rng, N, 128, 4 * T), "rt": same(f(rng, 128, 4 * N)), "w": f(rng, N, 128, 2048), "u": same(f(rng, 128, 4)), "v": f(rng, N, 128, 512)}
def planted(rng, a, b, own=1.0, off=1.0, way=1):
    d = setup_inputs(rng)
    at = np.arange(128) // (128 // N)
    big, mid = at[None, :, None] == a[:, None, :], at[None, :, None] == b[:, None, :]
    k = np.where(big, 16.0, np.where(mid, 4.0, 1.0))[..., None]
    g = np.where((big | mid)[..., None], 1, signs(rng, N, 128, T, 4))
    d["x"] = bf(sized(rng, N, 128, T, 4) * k * g).reshape(N, 128, 4 * T)
    d["rt"] = same(bf(sized(rng, 128, N, 4) * (at[:, None] == np.arange(N))[..., None]).reshape(128, 4 * N))
    d["w"] = bf(sized(rng, N, 128, 2048) * signs(rng, N, 128, 2048) * np.where(at == np.arange(N)[:, None], own, off)[..., None])
    d["u"] = same(bf(way * sized(rng, 128, 4)))
    return d
def setup_inputs_crowd(rng):
    a, b = np.zeros((N, T), int), np.zeros((N, T), int)
    for s in range(N):
        h, k = (s + (0, 1, 1)[s % 3]) % N, (s + (1, 0, 2)[s % 3]) % N
        rest = rng.permutation(np.array([e for e in range(N) if e not in (h, k)]))
        m, n = rest[np.arange(T) % rest.size], rest[np.arange(1, T + 1) % rest.size]
        p = rng.permutation(T)
        p[:CAPP + 16] = np.sort(p[:CAPP + 16])
        m[:CAPP + 16] = h
        m[CAPP + 16:CAPP + 16 + CAPR] = k
        n[np.concatenate([np.arange(CAPP + 16 + CAPR, T), np.arange(CAPP)])[:CAPP - CAPR]] = k
        a[s, p], b[s, p] = m, n
    return planted(rng, a, b, own=2.0 ** -4, way=-2.0 ** 24)
def setup_inputs_second(rng):
    a, b = np.zeros((N, T), int), np.zeros((N, T), int)
    one, i = int(rng.integers(0, N)), np.arange(T)
    half, last = CAPP // 2, CAPP + CAPP // 2 + 16
    for s in range(N):
        g = rng.permutation(N)
        h, k, rest = g[0], g[1], g[2:]
        m, n = rest[i % rest.size], rest[(i + 1) % rest.size]
        if s == one:
            m[:] = h
            n = g[1 + i % (N - 1)]
        else:
            m[:last] = h
            n[half:last] = k
        turn = (i + rng.integers(0, 2)) % 2 == 1
        p = rng.permutation(T)
        p[:last] = np.sort(p[:last])
        a[s, p], b[s, p] = np.where(turn, m, n), np.where(turn, n, m)
    return planted(rng, a, b, own=2.0 ** 4, way=-1)
def setup_inputs_ties(rng):
    kind = np.stack([rng.permutation(T) % N for s in range(N)])
    e = rng.integers(2, N, (N, T))
    a = np.where(kind == 0, 0, e)
    b = np.where(kind == 0, e, np.where(kind == 1, 0, e ^ 1))
    d = planted(rng, a, b)
    d["rt"][:, :, 4:8] = d["rt"][:, :, :4]
    d["w"][1::2] = d["w"][::2]
    d["w"][:2, :, :4] = 0
    d["w"][1, 128 // N, 0] = BF(4)
    return d
def setup_inputs_zero(rng):
    a = rng.integers(0, N, (N, T))
    b = (a + rng.integers(1, N, (N, T))) % N
    d = planted(rng, a, b, way=-1)
    at, late = np.arange(128) // (128 // N), np.arange(128) % (128 // N) >= 128 // N // 2
    kind = np.stack([rng.permutation(T) % 4 for s in range(N)])
    low = (at[None, :, None] == a[:, None, :]) & (kind % 2 == 1)[:, None, :] | (at[None, :, None] == b[:, None, :]) & (kind >= 2)[:, None, :]
    t = d["x"].astype(np.float32).reshape(N, 128, T, 4)
    d["x"] = bf(np.where(late[None, :, None, None], np.abs(t) * np.where(low, -1, 1)[..., None], t)).reshape(N, 128, 4 * T)
    d["rt"] = bf(d["rt"].astype(np.float32) * ~late[None, :, None])
    d["w"] = bf(np.abs(d["w"].astype(np.float32)) * ((at == np.arange(N)[:, None]) & late)[..., None])
    return d
def setup_inputs_spread(rng):
    return {**setup_inputs(rng), "x": wide(rng, N, 128, 4 * T, cols=6)}
def check_inputs(d):
    b = []
    for k in ("x", "rt", "w", "u", "v"):
        t = np.abs(d[k].astype(np.float32))
        if not (np.isfinite(t).all() and ((t == 0) | (t >= 2.0 ** -30) & (t <= 2.0 ** 30)).all()): b.append("a value of " + k)
    for k, n in (("rt", N), ("u", 1)):
        t = d[k].astype(np.float32)
        if (t[:, :, 4 * n:] != 0).any(): b.append(k + " has numbers behind its first columns")
        if (t != t[:1]).any(): b.append(k + " isn't the same on all ranks")
    return b
def reference(x, rt, w, u, v):
    q, a, b = [], [], []
    for s in range(N):
        q.append(mx_ref.quantize(np.ascontiguousarray(x[s])))
        z = mx_ref.matmul(mx_ref.quantize(np.ascontiguousarray(rt[s])), q[s])[:N] + np.float32(0)
        o = np.argsort(-z, axis=0, kind="stable")
        a.append(o[0])
        b.append(o[1])
    took = [[np.flatnonzero((a[s] == e) | (b[s] == e))[:CAPP] for e in range(N)] for s in range(N)]
    good = np.full((N, N, T), -np.inf, np.float32)
    made = []
    for e in range(N):
        t = join(*[pick(q[s], np.concatenate([took[s][e], np.full(CAPP - took[s][e].size, -1)])) for s in range(N)])
        rs = [mx_ref.matmul(mx_ref.quantize(np.ascontiguousarray(cut(w[e], i))), t) for i in range(4)]
        made.append(mx_ref.quantize(tile([np.maximum(k, np.float32(0)) * np.float32(0.0625) for k in rs])))
        z = mx_ref.matmul(mx_ref.quantize(np.ascontiguousarray(u[e])), made[e])[0] + np.float32(0)
        for s in range(N): good[s, e, took[s][e]] = z[s * CAPP:s * CAPP + took[s][e].size]
    every = join(*made)
    oc, osc = np.zeros((N, 128, 4 * T), np.uint8), np.zeros((N, 16, T), np.uint8)
    wn, y = np.zeros((N, 1, T), np.float32), np.zeros((N, 128, T), np.float32)
    for s in range(N):
        ga, gb = good[s, a[s], np.arange(T)], good[s, b[s], np.arange(T)]
        win = np.where(ga >= gb, a[s], b[s])
        none = np.maximum(ga, gb) == -np.inf
        wn[s, 0] = np.where(none, -100, -1 - win)
        at = np.full(T, -1)
        for e in range(N):
            home = np.flatnonzero((win == e) & ~none)[:CAPR]
            wn[s, 0, home] = e
            at[home] = (e * N + s) * CAPP + np.searchsorted(took[s][e], home)
        z = pick(every, at)
        oc[s], osc[s] = emit(z)
        y[s] = mx_ref.matmul(mx_ref.quantize(np.ascontiguousarray(v[s])), z)
    return {"oc": oc, "osc": osc, "wn": wn, "y": y}

@@ -1,0 +1,565 @@
+from concourse.bass import DstId, RemoteDMATransfer
+from concourse.mybir import dt, AluOpType as A, AxisListType, ActivationFunctionType as F
+
+C8, PL, BF, FP, I32, U16 = "float8_e4m3fn_x4", "uint8", "bfloat16", "float32", "int32", "uint16"
+CAPP, CAPR, DUMP, TOK, ZC = 48, 32, 32, 128, 16
+BIG = 2.0 ** 98
+SHAPES = {
+    C8: "xq144 rq128 rp128 wq512 uq128 up128 vq128 xg336 he128 xe144 hx192 lx336 hq336 hr192 hb480 hab272 zq128",
+    PL: "xs144 rs128 rps128 ws512 us128 ups128 vs128 xgs336 hes128 xes144 hxs192 lxs336 hqs336 hrs192 hbs480 habs272 zs128",
+    BF: "xt576 rtt512 wt2048 ut512 vt512 hto512 ht1344 vals32 nn128 nt128 win1056 ot768 ge128 kk128 ww128 cc128",
+    FP: "yb128 ya272 ff4 jr128 jra128 e_4 q_32 kv32 kvt32 kt8 ka8 c2_8 c3_8 sign64 z32 cw3 cr1 bs64 gt64 rk64 cs128 ct32 "
+        "un8 ta24 tb24 vm2 tk2 mm1 ra128 rb128 pa128 pb128 dt512 qb128 wa32 wb32",
+    I32: "ip1 ii4",
+    U16: "lp8 lo8 of2 od24 oh16 oz8 le4",
+}
+
+
+def _split(s):
+    k = len(s.rstrip("0123456789"))
+    return s[:k], int(s[k:])
+
+
+SCRATCH = {
+    "th": ("sbuf", [128, 2, 8], FP), "oh2": ("sbuf", [128, 2, 8], FP),
+    "pr": ("sbuf", [128, 2, 8], FP), "ph": ("sbuf", [128, 2, 8], FP), "dd": ("sbuf", [128, 8, 3, 2, 16], BF),
+    "zst": ("sbuf", [128, 5, 32], FP), "zt": ("sbuf", [128, 5, 32], FP), "rz": ("sbuf", [128, 5, 128], FP),
+    "d2": ("sbuf", [128, 2, 8, 2, 16], FP), "vv": ("sbuf", [128, 8, 2, 16], BF), "vvt": ("sbuf", [128, 8, 32], BF),
+    "lv": ("sbuf", [128, 8, 2, 16], BF), "lvt": ("sbuf", [128, 8, 32], BF), "wp": ("sbuf", [128, 8, 8], FP),
+    "pp": ("sbuf", [128, 8, 2, 16], FP), "ppt": ("sbuf", [128, 8, 32], FP), "vz": ("sbuf", [128, 8, 8], FP),
+    "gh": ("sbuf", [128, 4, 2, 32], BF), "ght": ("sbuf", [128, 4, 2, 32], BF),
+    "gs": ("sbuf", [128, 4, 32], BF), "gst": ("sbuf", [128, 4, 32], BF),
+    "psa": ("psum", [128, 2048], FP), "psb": ("psum", [128, 2048], FP),
+}
+for _t, _s in SHAPES.items():
+    for _w in _s.split():
+        SCRATCH[_split(_w)[0]] = ("sbuf", [128, _split(_w)[1]], _t)
+SEMAPHORES = ("v f gi ge1 gq gth gk gh ga sff sff2 swz scn srt sx sw su0 sv0 srq srp srps sxq mS sdd sde sod1 sod2 sg1 sg1s sg2 sg2s loc he de dl sep seps hd hret dsp dcr rsp rcr "
+              "suq sup sups swq sz so mo sro r1s r2s q1 q2 soh sba sbas sbb sbbs mqa mqb sww scc sgg sgs soz szq szs my sya sy swn fin svq srz srd sz2 gz scw sd2 ska sp1 "
+              "m0 m1 m2 m3 m4 m5 m6 m7").split()
+
+
+def rank_program(g, core, T, topo):
+    S = T.sem
+    ranks = list(T.cores)
+    N = len(ranks)
+    u8, u32, X = dt.uint8, dt.uint32, AxisListType.X
+
+    def order(r):
+        rot = [(r + k) % N for k in range(1, N)]
+        far = [q for q in rot if not topo.may_write(ranks[r], ranks[q])]
+        near = [q for q in rot if topo.may_write(ranks[r], ranks[q])]
+        return far, near
+
+    def pos(r, q):
+        far, near = order(r)
+        return (far + near + [r]).index(q)
+
+    def place(r, q):
+        far, near = order(r)
+        return (far + near).index(q)
+
+    def handers(r):
+        c = ranks[r]
+        can = [h for h in topo.cores_of(c) if h != c and all(topo.may_write(h, ranks[q]) for q in order(r)[0])]
+        can = sorted(can, key=lambda h: (topo.die(h) == topo.die(c), h))[:4]
+        return can + [h for h in topo.cores_of(c) if h != c and topo.die(h) == topo.die(c) and h not in can][:1]
+
+    def send(dst_core, es, sem, src, dst):
+        rid, pid = topo.addr(dst_core, core)
+        return RemoteDMATransfer(dst_ids=[DstId(rid=rid, pnc=pid)], dma_engine_mask=sum(1 << e for e in es), remote_sem=sem, src=src, dst=dst)
+
+    def cod(t, a, b):
+        return t[:, a:b].bitcast(u8)
+
+    def run(planes, c, p, a, b):
+        return p[:, a:b] if planes else cod(c, a, b)
+
+    def w32(t, a, b):
+        return t[:, a:b].bitcast(u32)
+
+    def share(es, k):
+        m = len(es) // (k if k < 3 else 4)
+        return [es[m * i:m * i + m] if i < k - 1 else es[m * i:] for i in range(k)]
+
+    def off(r):
+        return topo.engines(ranks[r], ranks[order(r)[1][0]])
+
+    def inside(r, k):
+        es = topo.engines(ranks[r], handers(r)[k])
+        return [e for e in es if e not in off(r)] if k == 4 else share(es, 2)[k % 2]
+
+    def ahead(r, k):
+        es, m = topo.engines(ranks[r], handers(r)[k]), len(inside(r, k)) // 2
+        return inside(r, k) if k == 4 else es[m * k:m * k + m]
+
+    rank = T.rank_of(core)
+
+    if rank is None:
+        mine = [r for r in range(N) if ranks[r] in topo.cores_of(core)]
+        if not mine or core not in handers(mine[0]):
+            return
+        r = mine[0]
+        far, near = order(r)
+        i = handers(r).index(core)
+        n = [0]
+
+        def hand(planes, sem_in, cnt, sem, bc, bp, dc, dp, jobs):
+            g.wait_ge(sem_in, cnt)
+            t = []
+            for es, (q, a, b, m) in zip(share(topo.engines(core, ranks[jobs[0][0]]), len(jobs)), jobs):
+                t.append(send(ranks[q], es, sem, run(planes, bc, bp, a, a + m), run(planes, dc, dp, b, b + m)))
+                n[0] += len(es)
+            g.remote_dma_fused(t, local_sem=S.loc)
+        m = TOK // 4
+        hand(i == 4, S.he, len(ahead(r, i)), S.de, T.he, T.hes, T.xe, T.xes, [(near[-1], 0, ZC, TOK) if i == 4 else (near[-1], 0, ZC + m * i, m)])
+        to, out, back, s_out, s_back = (near[:2], 2 * CAPP, CAPP, S.dsp, S.rsp) if i == 4 else (far[2 * (i % 2):2 * (i % 2) + 2], 0, 0, S.dcr, S.rcr)
+        hand(i >= 2, S.hd, len(inside(r, i)), s_out, T.hx, T.hxs, T.lx, T.lxs, [(q, out + CAPP * k, CAPP * place(q, r), CAPP) for k, q in enumerate(to)])
+        hand(i >= 2, S.hret, len(inside(r, i)), s_back, T.hr, T.hrs, T.hb, T.hbs, [(q, back + CAPP * k, ZC + CAPP * pos(q, r), CAPP) for k, q in enumerate(to)])
+        g.wait_ge(S.loc, n[0])
+        return
+
+    far, near = order(rank)
+    lists = far + [rank] + near
+    half, own, rest = CAPP * len(far), CAPP * (N - 1), CAPP * len(near)
+    origin = [q for q in near if order(q)[1][-1] == rank][0]
+
+    def share_of(q, k):
+        i = order(q)[1].index(rank)
+        return len(share(off(q), k)[i]) if i < k else 0
+    ahead_in = sum(len(topo.engines(h, core)) for h in handers(origin))
+    list_in = len(off(origin))
+    near_in = sum(2 * share_of(q, 2) for q in near)
+    near_back = sum(share_of(q, 3) + (share_of(q, 2) or share_of(q, 3)) for q in near)
+    far_in = sum(2 * len(share(topo.engines(handers(q)[0], core), 2)[0]) for q in far)
+    v, sc, te, sy = g.vector, g.scalar, g.tensor, g.sync
+    n, nf, nl = [0], [0], [0]
+
+    def op(c):
+        c.then_inc(S.v, 1)
+        n[0] += 1
+
+    def done():
+        v.wait_ge(S.v, n[0])
+
+    def fl(c):
+        c.then_inc(S.f, 1)
+        nf[0] += 1
+
+    def fdone():
+        v.wait_ge(S.f, nf[0])
+
+    def tt(*a):
+        op(v.tensor_tensor(*a))
+
+    def ts(*a):
+        op(v.tensor_scalar(*a))
+
+    def fused(t, *sems):
+        for s in sems:
+            g.wait_ge(s, 1)
+        g.remote_dma_fused([send(*a) for a in t], local_sem=S.loc)
+        nl[0] += sum(len(a[1]) for a in t)
+
+    def to_far(bc, bp, sem_c, sem_p, sem, dc, dp):
+        for planes in (False, True):
+            fused([(handers(rank)[2 * planes + i], inside(rank, 2 * planes + i), sem, run(planes, bc, bp, 96 * i, 96 * i + 96), run(planes, dc, dp, 0, 96))
+                   for i in range(2)], sem_p if planes else sem_c)
+
+    def to_near(to, first, bc, dc, sem):
+        t = []
+        for i, (q, b) in enumerate(to):
+            a = first + CAPP * i
+            t.append((ranks[q], share(off(rank), len(to))[i], sem, cod(bc, a, a + CAPP), cod(dc, b, b + CAPP)))
+        return t
+
+    sc.dma_start(T.rtt[:, 0:32], T.rt[:, 0:32]).then_inc(S.srt, 16)
+    sy.dma_start(T.xt[:, 4 * ZC:4 * ZC + 512], T.x[:]).then_inc(S.sx, 16)
+    sc.dma_start(T.wt[:], T.w[:]).then_inc(S.sw, 16)
+    sy.dma_start(T.ut[:], T.u[:]).then_inc(S.su0, 16)
+
+    def iota(out, pattern, base, sem):
+        g.iota(out, pattern, base, 0, allow_small_or_imprecise_dtypes=True).then_inc(sem, 1)
+
+    def columns(out, value, sem):
+        i, k = 0, 0
+        while i < N:
+            m = 1
+            while i + m < N and lists[i + m] == lists[i] + 2 * m and (m == 1 or value(lists[i + m]) - value(lists[i + m - 1]) == value(lists[i + 1]) - value(lists[i])):
+                m += 1
+            a, step = lists[i], value(lists[i + 1]) - value(lists[i]) if m > 1 else 0
+            iota(out[:, a:a + 2 * m - 1:2], [[step, m]], value(a), sem)
+            i, k = i + m, k + 1
+        return k
+    g.iota(T.ip[:], [[0, 1]], 0, 1).then_inc(S.gi, 1)
+    iota(T.e_[:], [[2, 4]], 0, S.ge1)
+    nk = columns(T.kv, lambda e: DUMP + TOK * lists.index(e) - 1, S.gk)
+    iota(T.kv[:, N:32], [[0, 32 - N]], 0, S.gk)
+    nk += 1
+    iota(T.th[:, 1, :], [[-1, 8]], 1, S.gth)
+    iota(T.th[:, 0, :], [[-1, 8]], 0, S.gth)
+    iota(T.q_[:], [[0, 2], [1, 16]], ZC, S.gq)
+
+    m = TOK // 4
+    fused([(handers(rank)[k], ahead(rank, k), S.he, cod(T.xq, ZC + m * k, ZC + m * k + m), cod(T.he, 0, m)) for k in range(4)], S.sxq)
+    fused([(handers(rank)[4], ahead(rank, 4), S.he, T.xs[:, ZC:ZC + TOK], T.hes[:, 0:TOK])])
+    iota(T.zst[:, 0:2, :], [[0, 2], [0, 32]], 0, S.gz)
+    iota(T.z[:], [[0, 32]], ZC - DUMP, S.gz)
+    na = columns(T.ka, lambda e: CAPP * pos(rank, e) - TOK * lists.index(e), S.ga)
+
+    op(v.memset(T.rtt[:, 32:512], 0.0))
+    v.wait_ge(S.gi, 1)
+    ts(T.ii[:, 0:1], T.ip[:], 7, None, A.bitwise_and)
+    ts(T.ii[:, 1:2], T.ip[:], 3, 1, A.logical_shift_right, A.bitwise_and)
+    fl(v.memset(T.xt[:, 0:4 * ZC], 0.0))
+    fl(v.memset(T.sign[:], 1.0))
+    done()
+    op(v.tensor_copy(T.ff[:, 0:2], T.ii[:, 0:2]))
+    fl(v.tensor_scalar(T.ii[:, 2:3], T.ip[:], 112, None, A.bitwise_and))
+    fl(v.tensor_scalar(T.ii[:, 3:4], T.ip[:], 31, None, A.bitwise_and))
+    v.wait_ge(S.ge1, 1)
+    done()
+    op(v.tensor_scalar(T.lp[:, 0:4], T.e_[:], T.ff[:, 1:2], T.ff[:, 0:1], A.add, A.max))
+    op(v.tensor_scalar(T.lp[:, 4:8], T.e_[:], T.ff[:, 1:2], T.ff[:, 0:1], A.add, A.min))
+    listed_pairs = n[0]
+    fdone()
+    v.tensor_copy(T.ff[:, 2:4], T.ii[:, 2:4]).then_inc(S.sff, 1)
+    fl(v.memset(T.sign[:, 0:64:9], -1.0))
+
+    v.wait_ge(S.srt, 16)
+    done()
+    v.quantize_mx(T.rq[:], T.rs[:], T.rtt[:]).then_inc(S.srq, 1)
+    fdone()
+    fl(v.memset(T.sign[:, 0:64:8], 0.0))
+    v.wait_ge(S.srq, 1)
+    v.tensor_copy(w32(T.rp, 0, 128), w32(T.rq, 0, 128).indirect(T.lp[:])).then_inc(S.srp, 1)
+    sc.wait_ge(S.v, 1)
+    sc.activation(T.win[:, 0:480], T.rtt[:, 32:512], F.Copy).then_inc(S.swz, 1)
+    sc.wait_ge(S.srq, 1)
+    sc.wait_ge(S.v, listed_pairs)
+    sc.activation(T.rps[:, 0:128], T.rs[:, 0:128].indirect(T.lp[:]), F.Copy).then_inc(S.srps, 1)
+    sc.activation(T.win[:, 480:960], T.rtt[:, 32:512], F.Copy).then_inc(S.swz, 1)
+    sc.activation(T.win[:, 960:1056], T.rtt[:, 32:128], F.Copy).then_inc(S.swz, 1)
+    sc.wait_ge(S.sff, 1)
+    sc.wait_ge(S.gq, 1)
+    sc.activation(T.vals[:], T.q_[:], F.Identity, bias=T.ff[:, 2:3]).then_inc(S.scn, 1)
+    sc.wait_ge(S.gk, nk)
+    sc.activation(T.kt[:], T.kv[:, 0:8], F.Copy, bias=1.0 * CAPP).then_inc(S.scn, 1)
+    sc.activation(T.cw[:, 0:1], T.ff[:, 3:4], F.Copy, bias=0.5).then_inc(S.scw, 1)
+    sc.activation(T.cr[:], T.ff[:, 3:4], F.Relu, scale=100.0, bias=-100.0 * (N - 2)).then_inc(S.scw, 1)
+    sc.wait_ge(S.scw, 2)
+    sc.activation(T.cw[:, 2:3], T.cr[:], F.Copy, scale=-1.0).then_inc(S.scw, 1)
+    v.wait_ge(S.sx, 16)
+    v.quantize_mx(T.xq[:], T.xs[:], T.xt[:]).then_inc(S.sxq, 1)
+    te.wait_ge(S.srp, 1)
+    te.wait_ge(S.srps, 1)
+    te.wait_ge(S.sxq, 1)
+    te.matmul_mx(T.psb[:, 0:128], T.xq[:, ZC:ZC + TOK], T.xs[:, ZC:ZC + TOK], T.rp[:, 0:128], T.rps[:, 0:128], True, True).then_inc(S.mS, 1)
+    op(v.memset(T.nn[:], 0.0))
+    v.wait_ge(S.gk, nk)
+    op(v.transpose(T.kvt[:], T.kv[:]))
+    op(v.memset(T.lo[:], 0))
+
+    v.wait_ge(S.mS, 1)
+    op(v.tensor_copy(T.bs[:], T.psb[:, 64:128]))
+    done()
+    tt(T.gt[:], T.psb[:, 0:64], T.bs[:], A.is_gt)
+    fdone()
+    done()
+    op(v.tensor_tensor_scan(T.rk[:], T.sign[:], T.gt[:], 0.0, A.mult, A.add))
+    v.wait_ge(S.gth, 2)
+    done()
+    for d, b, p, c in ((64, 0, 64, 0), (32, 0, 32, 0), (64, 32, 32, 32), (96, 0, 32, 32), (96, 64, 32, 64), (0, 0, 128, 96)):
+        tt(T.nn[d:d + p, c:c + 8], T.rk[b:b + p, 7:64:8], T.th[b:b + p, 1, :], A.is_le)
+    for k in range(2):
+        fl(v.tensor_tensor(T.oh2[:, k, :], T.rk[:, 7:64:8], T.th[:, k, :], A.is_equal))
+    done()
+    op(v.transpose(T.nt[:], T.nn[:]))
+    done()
+    op(v.tensor_tensor_scan(T.cs[:], T.nt[:], T.nt[:], T.kvt[:, 0:1], A.add, A.max))
+    done()
+    op(v.transpose(T.ct[:], T.cs[:, 96:128]))
+    fdone()
+    done()
+    for k in range(2):
+        tt(T.pr[:, k, :], T.oh2[:, k, :], T.ct[:, 0:8], A.mult)
+    done()
+    op(v.tensor_reduce(T.of[:], T.pr[:], X, A.max))
+    v.wait_ge(S.scn, 2)
+    fl(v.tensor_tensor(T.un[:], T.ct[:, 0:8], T.kt[:], A.is_le))
+    v.wait_ge(S.swz, 3)
+    done()
+    op(v.tensor_copy(T.win[:].indirect(T.of[:]), T.vals[:]))
+    v.wait_ge(S.ga, na)
+    fl(v.tensor_tensor(T.c3_[:], T.ct[:, 0:8], T.ka[:], A.add))
+    done()
+    scattered = n[0]
+
+    def lay(i, d):
+        return T.dd[:, i, :, d, :], T.win[:, DUMP + TOK * i:DUMP + TOK * i + CAPP]
+    sc.wait_ge(S.v, scattered)
+    for i in range(8):
+        if i != 3:
+            sc.activation(*lay(i, 1), F.Copy).then_inc(S.sde if i > 3 else S.sdd, 1)
+    for i in range(4):
+        op(v.tensor_copy(*lay(i, 0)))
+    op(v.tensor_copy(*lay(3, 1)))
+    fl(v.tensor_copy(*lay(4, 0)))
+    v.wait_ge(S.sdd, 3)
+    done()
+    op(v.transpose(T.ot[:, 0:384], T.dd[:, 0:4]))
+    fl(v.tensor_copy(*lay(5, 0)))
+    fl(v.tensor_copy(*lay(6, 0)))
+    done()
+    tt(T.ta[:, 0:12], T.ot[:, 0:384:32], T.ot[:, 16:384:32], A.add)
+    fl(v.tensor_copy(*lay(7, 0)))
+    done()
+    tt(T.tb[0:64, 0:12], T.ta[0:64, 0:12], T.ta[64:128, 0:12], A.add)
+    v.wait_ge(S.sde, 4)
+    fdone()
+    done()
+    for p in (0, 32):
+        tt(T.od[p:p + 32, 0:12], T.tb[0:32, 0:12], T.tb[32:64, 0:12], A.add)
+    done()
+    far_list = n[0]
+    v.tensor_copy(T.od[64:128, 0:12], T.od[0:64, 0:12]).then_inc(S.sod1, 1)
+    fl(v.transpose(T.ot[:, 384:768], T.dd[:, 4:8]))
+
+    def picked(lo, hi, a, s1, s2):
+        b = a + 16 * (hi - lo)
+        v.tensor_copy(w32(T.xg, a, b), w32(T.xq, 0, ZC + TOK).indirect(T.od[:, lo:hi])).then_inc(s1, 1)
+        sc.activation(T.xgs[:, a:b], T.xs[:, 0:ZC + TOK].indirect(T.od[:, lo:hi]), F.Copy).then_inc(s2, 1)
+    v.wait_ge(S.sod1, 1)
+    sc.wait_ge(S.sod1, 1)
+    sc.wait_ge(S.v, far_list)
+    picked(0, 12, 0, S.sg1, S.sg1s)
+    fdone()
+    tt(T.ta[:, 12:24], T.ot[:, 384:768:32], T.ot[:, 400:768:32], A.add)
+    fl(v.tensor_tensor(T.c2_[:], T.un[:], T.c3_[:], A.mult))
+    done()
+    tt(T.tb[0:64, 12:24], T.ta[0:64, 12:24], T.ta[64:128, 12:24], A.add)
+    done()
+    for p in (0, 32):
+        tt(T.od[p:p + 32, 12:24], T.tb[0:32, 12:24], T.tb[32:64, 12:24], A.add)
+    done()
+    near_list = n[0]
+    v.tensor_copy(T.od[64:128, 12:24], T.od[0:64, 12:24]).then_inc(S.sod2, 1)
+    v.wait_ge(S.sod2, 1)
+    sc.wait_ge(S.sod2, 1)
+    sc.wait_ge(S.v, near_list)
+    picked(12, 21, half, S.sg2, S.sg2s)
+
+    to_far(T.xg, T.xgs, S.sg1, S.sg1s, S.hd, T.hx, T.hxs)
+    g.wait_ge(S.sod2, 1)
+    g.wait_ge(S.v, near_list)
+    fused([(ranks[near[2]], off(rank), S.dl, T.od[:, 21:24], T.le[:, 0:3])])
+    fused(to_near([(q, CAPP * place(q, rank)) for q in near[:2]], half + CAPP, T.xg, T.lx, S.dsp)
+          + [(handers(rank)[4], inside(rank, 4), S.hd, T.xgs[:, half - CAPP:half + 3 * CAPP], T.hxs[:, 0:4 * CAPP])], S.sg2, S.sg2s)
+    iota(T.jr[:], [[1, 128]], ZC, S.gh)
+    iota(T.jra[:], [[1, 128]], ZC + TOK, S.gh)
+    iota(T.wa[:], [[0, 32]], 0, S.gh)
+
+    v.wait_ge(S.sw, 16)
+    for i in range(4):
+        v.quantize_mx(T.wq[:, 128 * i:128 * i + 128], T.ws[:, 128 * i:128 * i + 128], T.wt[:, 512 * i:512 * i + 512]).then_inc(S.swq, 1)
+
+    te.wait_ge(S.sg2, 1)
+    te.wait_ge(S.sg2s, 1)
+    for i in range(4):
+        te.wait_ge(S.swq, i + 1)
+        te.matmul_mx(T.psa[:, 512 * i:512 * i + 128], T.wq[:, 128 * i:128 * i + 128], T.ws[:, 128 * i:128 * i + 128],
+                     T.xg[:, half:half + 128], T.xgs[:, half:half + 128], True, True).then_inc(S.mo, 1)
+    for i in range(4):
+        sc.wait_ge(S.mo, i + 1)
+        sc.activation(T.hto[:, i:512:4], T.psa[:, 512 * i:512 * i + 128], F.Relu, scale=0.0625).then_inc(S.sro, 1)
+
+    fdone()
+    for k in range(2):
+        tt(T.ph[:, k, :], T.oh2[:, k, :], T.c2_[:], A.mult)
+    v.wait_ge(S.gz, 2)
+    for k in range(2):
+        fl(v.tensor_tensor(T.zst[:, k, 0:8], T.oh2[:, k, :], T.un[:], A.mult))
+    done()
+    op(v.tensor_reduce(T.vm[:], T.ph[:], X, A.max))
+    done()
+    ts(T.tk[:], T.vm[:], 0.0, BIG, A.is_gt, A.mult)
+    for k in range(2):
+        fl(v.tensor_scalar(T.zst[:, 3 + k, :], T.z[:], T.vm[:, k:k + 1], 0.0, A.add, A.max))
+    done()
+    tt(T.mm[:, 0:1], T.tk[:, 1:2], T.tk[:, 0:1], A.subtract)
+    done()
+    ts(T.zst[:, 2, :], T.z[:], 0.0, T.mm[:, 0:1], A.mult, A.add)
+    fdone()
+    done()
+    op(v.transpose(T.zt[:], T.zst[:]))
+    sc.wait_ge(S.v, n[0])
+    for b in range(4):
+        sc.activation(T.rz[0:32, :, 32 * b:32 * b + 32], T.zt[32 * b:32 * b + 32, :, :], F.Copy).then_inc(S.srz, 1)
+    sy.wait_ge(S.srz, 4)
+    for b in range(1, 4):
+        sy.dma_start(T.rz[32 * b:32 * b + 32, :, :], T.rz[0:32, :, :]).then_inc(S.srd, 16)
+
+    a = CAPP * place(rank, origin)
+    op(v.tensor_copy(w32(T.xe, 0, ZC), w32(T.xq, 0, ZC + TOK).indirect(T.lo[:, 0:1])))
+    sc.activation(T.xes[:, 0:ZC], T.xs[:, 0:ZC + TOK].indirect(T.lo[:, 0:1]), F.Copy).then_inc(S.sz, 1)
+    v.wait_ge(S.sro, 4)
+    v.quantize_mx(T.hb[:, ZC + own:ZC + own + 128], T.hbs[:, ZC + own:ZC + own + 128], T.hto[:]).then_inc(S.so, 1)
+    done()
+    sc.wait_ge(S.sz, 1)
+    for q in (v, sc):
+        q.wait_ge(S.de, ahead_in)
+        q.wait_ge(S.dl, list_in)
+    v.tensor_copy(w32(T.lx, a, a + CAPP), w32(T.xe, 0, ZC + TOK).indirect(T.le[:, 0:3])).then_inc(S.sep, 1)
+    sc.activation(T.lxs[:, a:a + CAPP], T.xes[:, 0:ZC + TOK].indirect(T.le[:, 0:3]), F.Copy).then_inc(S.seps, 1)
+
+    def expert(h):
+        a, m = (0, half) if h else (half, rest)
+        ps, t0, rs = (T.psb, 0, S.r2s) if h else (T.psa, 4 * half, S.r1s)
+        if h:
+            te.wait_ge(S.dcr, far_in)
+        else:
+            te.wait_ge(S.sro, 4)
+            te.wait_ge(S.dsp, near_in)
+            te.wait_ge(S.sep, 1)
+            te.wait_ge(S.seps, 1)
+        for i in range(4):
+            te.matmul_mx(ps[:, 512 * i:512 * i + m], T.wq[:, 128 * i:128 * i + 128], T.ws[:, 128 * i:128 * i + 128],
+                         T.lx[:, a:a + m], T.lxs[:, a:a + m], True, True).then_inc(S["m%d" % (4 * h + i)], 1)
+        for i in range(4):
+            src, dst = ps[:, 512 * i:512 * i + m], T.ht[:, t0 + i:t0 + 4 * m:4]
+            vec = i == 3 or h and i == 1
+            q = v if vec else sc
+            q.wait_ge(S["m%d" % (4 * h + i)], 1)
+            if vec:
+                ts(dst, src, 0.0, 0.0625, A.max, A.mult)
+            else:
+                sc.activation(dst, src, F.Relu, scale=0.0625).then_inc(rs, 1)
+        v.wait_ge(rs, 2 if h else 3)
+        done()
+        v.quantize_mx(T.hq[:, a:a + m], T.hqs[:, a:a + m], T.ht[:, t0:t0 + 4 * m]).then_inc(S.q2 if h else S.q1, 1)
+
+    expert(1)
+    to_far(T.hq, T.hqs, S.q2, S.q2, S.hret, T.hr, T.hrs)
+    expert(0)
+    fused(to_near([(q, ZC + CAPP * pos(q, rank)) for q in near], half, T.hq, T.hb, S.rsp)
+          + [(handers(rank)[4], inside(rank, 4), S.hret, T.hqs[:, half - CAPP:half + rest], T.hrs[:, 0:half])], S.q1)
+    a, b = half + 2 * CAPP, ZC + CAPP * pos(near[2], rank)
+    fused([(ranks[near[2]], share(off(rank), 3)[2], S.rsp, T.hqs[:, a:a + CAPP], T.hbs[:, b:b + CAPP])])
+    sy.wait_ge(S.dsp, near_in)
+    sy.dma_start(T.vt[:], T.v[:]).then_inc(S.sv0, 16)
+
+    v.wait_ge(S.su0, 16)
+    v.quantize_mx(T.uq[:], T.us[:], T.ut[:]).then_inc(S.suq, 1)
+    for q_, s_ in ((T.hb, T.hbs), (T.hab, T.habs)):
+        op(v.tensor_copy(w32(q_, 0, ZC), w32(T.xq, 0, ZC + TOK).indirect(T.lo[:, 0:1])))
+        sc.activation(s_[:, 0:ZC], T.xs[:, 0:ZC + TOK].indirect(T.lo[:, 0:1]), F.Copy).then_inc(S.sz2, 1)
+    v.wait_ge(S.suq, 1)
+    v.tensor_copy(w32(T.up, 0, 128), w32(T.uq, 0, 128).indirect(T.lo[:])).then_inc(S.sup, 1)
+    sc.wait_ge(S.srz, 4)
+    sc.wait_ge(S.srd, 48)
+    for k in range(2):
+        for d in range(2):
+            sc.activation(T.d2[:, k, :, d, :], T.rz[:, 3 + k, :], F.Copy).then_inc(S.sd2, 1)
+    sc.wait_ge(S.suq, 1)
+    sc.activation(T.ups[:, 0:128], T.us[:, 0:128].indirect(T.lo[:]), F.Copy).then_inc(S.sups, 1)
+    sc.activation(T.ra[:], T.rz[:, 0, :], F.Copy, scale=-6.0, bias=7.0).then_inc(S.ska, 1)
+    sc.activation(T.rb[:], T.rz[:, 1, :], F.Copy, scale=-7.0).then_inc(S.ska, 1)
+    v.wait_ge(S.srz, 4)
+    v.wait_ge(S.srd, 48)
+    v.wait_ge(S.gh, 3)
+    tt(T.pa[:], T.rz[:, 0, :], T.jr[:], A.mult)
+    tt(T.pb[:], T.rz[:, 1, :], T.jra[:], A.mult)
+    v.wait_ge(S.sd2, 4)
+    op(v.transpose(T.dt[:], T.d2[:]))
+    done()
+    tt(T.pp[:, :, 0, :], T.pa[:], T.pb[:], A.add)
+    sc.wait_ge(S.v, n[0])
+    sc.activation(T.pp[:, :, 1, :], T.pp[:, :, 0, :], F.Copy).then_inc(S.sp1, 1)
+    v.tensor_copy(T.oh[:], T.dt[:, 0:512:32]).then_inc(S.soh, 1)
+    v.wait_ge(S.sv0, 16)
+    v.quantize_mx(T.vq[:], T.vs[:], T.vt[:]).then_inc(S.svq, 1)
+    v.wait_ge(S.ska, 2)
+    tt(T.kk[:], T.ra[:], T.rb[:], A.add)
+    v.wait_ge(S.sp1, 1)
+    done()
+    op(v.transpose(T.ppt[:], T.pp[:]))
+    done()
+
+    for q in (v, sc):
+        q.wait_ge(S.soh, 1)
+        q.wait_ge(S.so, 1)
+        q.wait_ge(S.rsp, near_back)
+        q.wait_ge(S.rcr, far_in)
+    sc.wait_ge(S.sz2, 2)
+    for k, s1, s2 in ((1, S.sbb, S.sbbs), (0, S.sba, S.sbas)):
+        a = ZC + TOK * k
+        v.tensor_copy(w32(T.hab, a, a + 128), w32(T.hb, 0, 480).indirect(T.oh[:, 8 * k:8 * k + 8])).then_inc(s1, 1)
+        sc.activation(T.habs[:, a:a + 128], T.hbs[:, 0:480].indirect(T.oh[:, 8 * k:8 * k + 8]), F.Copy).then_inc(s2, 1)
+    for s in (S.sup, S.sups, S.svq, S.sbb, S.sbbs):
+        te.wait_ge(s, 1)
+    te.matmul_mx(T.psa[:, 0:128], T.up[:, 0:128], T.ups[:, 0:128], T.hab[:, ZC + TOK:ZC + 2 * TOK], T.habs[:, ZC + TOK:ZC + 2 * TOK], True, True).then_inc(S.mqb, 1)
+    te.wait_ge(S.sba, 1)
+    te.wait_ge(S.sbas, 1)
+    te.matmul_mx(T.psa[:, 512:640], T.up[:, 0:128], T.ups[:, 0:128], T.hab[:, ZC:ZC + TOK], T.habs[:, ZC:ZC + TOK], True, True).then_inc(S.mqa, 1)
+    te.matmul_mx(T.psa[:, 1024:1296], T.vq[:, 0:128], T.vs[:, 0:128], T.hab[:, 0:272], T.habs[:, 0:272], True, True).then_inc(S.my, 1)
+    v.wait_ge(S.mqb, 1)
+    tt(T.qb[:], T.psa[:, 0:128], T.rz[:, 2, :], A.add)
+    v.wait_ge(S.mqa, 1)
+    done()
+    tt(T.ge[:], T.psa[:, 512:640], T.qb[:], A.is_ge)
+    done()
+    v.tensor_tensor(T.ww[:], T.ge[:], T.kk[:], A.is_equal).then_inc(S.sww, 1)
+    v.wait_ge(S.sww, 1)
+    v.tensor_tensor_scan(T.cc[:], T.ww[:], T.ww[:], 0.0, A.add, A.max).then_inc(S.scc, 1)
+    for d in range(2):
+        fl(v.tensor_copy(T.vv[:, :, d, :], T.ww[:]))
+    v.wait_ge(S.scc, 1)
+    for d in range(2):
+        ts(T.lv[:, :, d, :], T.cc[:], 1.0 * CAPR, None, A.is_le)
+    fdone()
+    fl(v.transpose(T.vvt[:], T.vv[:]))
+    done()
+    op(v.transpose(T.lvt[:], T.lv[:]))
+    fdone()
+    fl(v.tensor_tensor(T.wp[:], T.vvt[:, :, 0:8], T.ppt[:, :, 0:8], A.mult))
+    v.wait_ge(S.sgg, 2)
+    op(v.transpose(T.ght[:], T.gh[:]))
+    fdone()
+    done()
+    fl(v.tensor_tensor(T.vz[:], T.wp[:], T.lvt[:, :, 0:8], A.mult))
+    v.wait_ge(S.sgs, 1)
+    op(v.transpose(T.gst[:], T.gs[:]))
+    fdone()
+    v.tensor_reduce(T.oz[:], T.vz[:], X, A.max).then_inc(S.soz, 1)
+    done()
+    tt(T.ght[:, :, 0, 8:16], T.ght[:, :, 1, 0:8], T.gst[:, :, 0:8], A.mult)
+    sc.wait_ge(S.my, 1)
+    sc.activation(T.ya[:], T.psa[:, 1024:1296], F.Copy).then_inc(S.sya, 1)
+    sc.wait_ge(S.scw, 3)
+    sc.wait_ge(S.sww, 1)
+    sc.activation(T.gh[:, :, 0, :], T.ww[:], F.Identity, scale=99.5, bias=T.cw[:, 2:3]).then_inc(S.sgg, 1)
+    sc.activation(T.gh[:, :, 1, :], T.ww[:], F.Copy, scale=T.cw[:, 0:1]).then_inc(S.sgg, 1)
+    sc.wait_ge(S.scc, 1)
+    sc.activation(T.gs[:], T.cc[:], F.Sign, scale=-1.0, bias=CAPR + 0.5).then_inc(S.sgs, 1)
+    v.wait_ge(S.soz, 1)
+    v.tensor_copy(w32(T.zq, 0, 128), w32(T.hab, 0, 272).indirect(T.oz[:])).then_inc(S.szq, 1)
+    v.tensor_copy(T.zs[:, 0:128], T.habs[:, 0:272].indirect(T.oz[:])).then_inc(S.szs, 1)
+    sc.wait_ge(S.sya, 1)
+    sc.wait_ge(S.soz, 1)
+    sc.activation(T.yb[:], T.ya[:, 0:272].indirect(T.oz[:]), F.Copy).then_inc(S.sy, 1)
+    done()
+    op(v.tensor_reduce(T.wa[:, 0:4], T.ght[:, :, 0, 0:16], X, A.add))
+    done()
+    v.transpose(T.wb[:], T.wa[:]).then_inc(S.swn, 1)
+    sy.wait_ge(S.szq, 1)
+    sy.dma_start(T.oc[:, 0:512], cod(T.zq, 0, 128)).then_inc(S.fin, 16)
+    sy.wait_ge(S.sy, 1)
+    sy.dma_start(T.y[:], T.yb[:]).then_inc(S.fin, 16)
+    for k in range(4):
+        q = sc if k % 2 else sy
+        q.wait_ge(S.szs, 1)
+        q.dma_start(T.osc[4 * k:4 * k + 4, 0:128], T.zs[32 * k:32 * k + 4, 0:128]).then_inc(S.fin, 16)
+    sy.wait_ge(S.swn, 1)
+    sy.dma_start(T.wn[0:1, 0:128], T.wb[0:4, 0:32]).then_inc(S.fin, 16)
+    sy.wait_ge(S.fin, 112)
+    g.wait_ge(S.loc, nl[0])

@@ -2,14 +2,16 @@ from concourse.bass import DstId, RemoteDMATransfer
 from concourse.mybir import dt, AluOpType as A, AxisListType, ActivationFunctionType as F
 
 C8, PL, BF, FP, I32, U16 = "float8_e4m3fn_x4", "uint8", "bfloat16", "float32", "int32", "uint16"
-CAPP, CAPR, DUMP, TOK, ZC = 48, 32, 32, 128, 16
-BIG = 2.0 ** 98
+CAPP, CAPR, TOK, ZC = 48, 32, 128, 16
+BIG, TINY, LOST, MID = 2.0 ** 98, 2.0 ** -120, 4096.0, 256
+PLACES = 2 * TOK
+OUT = 2 * TOK
+ALL = ZC + 2 * TOK + OUT
 SHAPES = {
-    C8: "xq144 rq128 rp128 wq512 uq128 up128 vq128 xg336 he128 xe144 hx192 lx336 hq336 hr192 hb480 hab272 zq128",
-    PL: "xs144 rs128 rps128 ws512 us128 ups128 vs128 xgs336 hes128 xes144 hxs192 lxs336 hqs336 hrs192 hbs480 habs272 zs128",
-    BF: "xt576 rtt512 wt2048 ut512 vt512 hto512 ht1344 vals32 nn128 nt128 win1056 ot768 ge128 kk128 ww128 cc128",
-    FP: "yb128 ya272 ff4 jr128 jra128 e_4 q_32 kv32 kvt32 kt8 ka8 c2_8 c3_8 sign64 z32 cw3 cr1 bs64 gt64 rk64 cs128 ct32 "
-        "un8 ta24 tb24 vm2 tk2 mm1 ra128 rb128 pa128 pb128 dt512 qb128 wa32 wb32",
+    C8: "xq144 rq128 rn128 rp256 wq512 uq128 up128 vq128 xg384 he128 xe144 hx192 lx288 hp128 hq320 ho128 hr96 hb480 hab528 zq128",
+    PL: "xs144 rs128 rns128 rps256 ws512 us128 ups128 vs128 xgs384 hes128 xes144 hxs192 lxs288 hpp128 hqs320 hos128 hps48 hrs192 hbs480 habs528 zs128",
+    BF: "xt576 rtt704 wt2048 vt512 hto512 ht1152 vals32 win1280 nn128 nt128 on128 cs128 ct32 ot768 ge128 ww128 cc128 wr528",
+    FP: "yb128 ya528 wb128 ff4 sb3 e_4 q_32 kb8 ka8 en8 c2_8 c3_8 dj64 thr64 cnt8 un8 ub8 nu8 sd8 ta24 tb24 qb128",
     I32: "ip1 ii4",
     U16: "lp8 lo8 of2 od24 oh16 oz8 le4",
 }
@@ -21,22 +23,21 @@ def _split(s):
 
 
 SCRATCH = {
-    "th": ("sbuf", [128, 2, 8], FP), "oh2": ("sbuf", [128, 2, 8], FP),
-    "pr": ("sbuf", [128, 2, 8], FP), "ph": ("sbuf", [128, 2, 8], FP), "dd": ("sbuf", [128, 8, 3, 2, 16], BF),
-    "zst": ("sbuf", [128, 5, 32], FP), "zt": ("sbuf", [128, 5, 32], FP), "rz": ("sbuf", [128, 5, 128], FP),
-    "d2": ("sbuf", [128, 2, 8, 2, 16], FP), "vv": ("sbuf", [128, 8, 2, 16], BF), "vvt": ("sbuf", [128, 8, 32], BF),
+    "gt": ("sbuf", [128, 8, 8], BF), "oh2": ("sbuf", [128, 2, 8], FP), "mk": ("sbuf", [128, 2, 8], FP),
+    "pr": ("sbuf", [128, 2, 8], FP), "ph": ("sbuf", [128, 5, 8], FP), "dd": ("sbuf", [128, 12, 2, 16, 2], BF),
+    "zst": ("sbuf", [128, 2, 32], FP), "zt": ("sbuf", [128, 2, 32], FP), "rz": ("sbuf", [128, 2, 128], BF),
+    "d2": ("sbuf", [128, 8, 2, 16], BF), "dt": ("sbuf", [128, 8, 32], BF), "jw": ("sbuf", [128, 8, 8], FP), "j0": ("sbuf", [128, 8, 8], FP),
+    "vv": ("sbuf", [128, 8, 2, 16], BF), "vvt": ("sbuf", [128, 8, 32], BF),
     "lv": ("sbuf", [128, 8, 2, 16], BF), "lvt": ("sbuf", [128, 8, 32], BF), "wp": ("sbuf", [128, 8, 8], FP),
-    "pp": ("sbuf", [128, 8, 2, 16], FP), "ppt": ("sbuf", [128, 8, 32], FP), "vz": ("sbuf", [128, 8, 8], FP),
-    "gh": ("sbuf", [128, 4, 2, 32], BF), "ght": ("sbuf", [128, 4, 2, 32], BF),
-    "gs": ("sbuf", [128, 4, 32], BF), "gst": ("sbuf", [128, 4, 32], BF),
+    "ppt": ("sbuf", [128, 8, 8], FP), "vz": ("sbuf", [128, 8, 9], FP),
     "psa": ("psum", [128, 2048], FP), "psb": ("psum", [128, 2048], FP),
 }
 for _t, _s in SHAPES.items():
     for _w in _s.split():
         SCRATCH[_split(_w)[0]] = ("sbuf", [128, _split(_w)[1]], _t)
-SEMAPHORES = ("v f gi ge1 gq gth gk gh ga sff sff2 swz scn srt sx sw su0 sv0 srq srp srps sxq mS sdd sde sod1 sod2 sg1 sg1s sg2 sg2s loc he de dl sep seps hd hret dsp dcr rsp rcr "
-              "suq sup sups swq sz so mo sro r1s r2s q1 q2 soh sba sbas sbb sbbs mqa mqb sww scc sgg sgs soz szq szs my sya sy swn fin svq srz srd sz2 gz scw sd2 ska sp1 "
-              "m0 m1 m2 m3 m4 m5 m6 m7").split()
+SEMAPHORES = ("v f gi ge1 gq gth gk gh ga sff swz scn srt sng sx sx0 sw su0 sv0 srq srp srps srz0 sxq mS snn sdd sde sg0 sg1 sg1s sg2 sg2s loc he he1 he2 de dl sep seps hd hret dsp dcr rsp rcr "
+              "suq sup sups swq sz so so1 sro r1s r2s q1 q2 q3 soh sba sbas sbb sbbs mqa mqb sww scc svv soz szq szs my sya sy swr swn fin svq srz srd sz2 sz3 gz sd2 sjw ssb "
+              "m0 m1 m2 m3 m4 m5 m6 m7 m8 m9 m10 m11").split()
 
 
 def rank_program(g, core, T, topo):
@@ -55,9 +56,14 @@ def rank_program(g, core, T, topo):
         far, near = order(r)
         return (far + near + [r]).index(q)
 
+    def origin_of(r):
+        return [q for q in order(r)[1] if order(q)[1][-1] == r][0]
+
+    def late_of(r):
+        return [q for q in order(r)[1] if q != origin_of(r)]
+
     def place(r, q):
-        far, near = order(r)
-        return (far + near).index(q)
+        return (order(r)[0] + late_of(r)).index(q)
 
     def handers(r):
         c = ranks[r]
@@ -79,19 +85,18 @@ def rank_program(g, core, T, topo):
         return t[:, a:b].bitcast(u32)
 
     def share(es, k):
-        m = len(es) // (k if k < 3 else 4)
-        return [es[m * i:m * i + m] if i < k - 1 else es[m * i:] for i in range(k)]
+        m = len(es) // k
+        return [es[m * i:m * i + m] for i in range(k)]
 
     def off(r):
         return topo.engines(ranks[r], ranks[order(r)[1][0]])
 
     def inside(r, k):
         es = topo.engines(ranks[r], handers(r)[k])
-        return [e for e in es if e not in off(r)] if k == 4 else share(es, 2)[k % 2]
+        return [e for e in es if e not in off(r)] if k == 4 else es if k < 2 else share(es, 2)[k % 2]
 
     def ahead(r, k):
-        es, m = topo.engines(ranks[r], handers(r)[k]), len(inside(r, k)) // 2
-        return inside(r, k) if k == 4 else es[m * k:m * k + m]
+        return inside(r, k) if k == 4 else share(topo.engines(ranks[r], handers(r)[k]), 4)[k]
 
     rank = T.rank_of(core)
 
@@ -111,26 +116,30 @@ def rank_program(g, core, T, topo):
                 t.append(send(ranks[q], es, sem, run(planes, bc, bp, a, a + m), run(planes, dc, dp, b, b + m)))
                 n[0] += len(es)
             g.remote_dma_fused(t, local_sem=S.loc)
-        m = TOK // 4
+        m, cnt = TOK // 4, len(inside(r, i))
         hand(i == 4, S.he, len(ahead(r, i)), S.de, T.he, T.hes, T.xe, T.xes, [(near[-1], 0, ZC, TOK) if i == 4 else (near[-1], 0, ZC + m * i, m)])
-        to, out, back, s_out, s_back = (near[:2], 2 * CAPP, CAPP, S.dsp, S.rsp) if i == 4 else (far[2 * (i % 2):2 * (i % 2) + 2], 0, 0, S.dcr, S.rcr)
-        hand(i >= 2, S.hd, len(inside(r, i)), s_out, T.hx, T.hxs, T.lx, T.lxs, [(q, out + CAPP * k, CAPP * place(q, r), CAPP) for k, q in enumerate(to)])
-        hand(i >= 2, S.hret, len(inside(r, i)), s_back, T.hr, T.hrs, T.hb, T.hbs, [(q, back + CAPP * k, ZC + CAPP * pos(q, r), CAPP) for k, q in enumerate(to)])
+        to, out, s_out = (near[:2], CAPP, S.dsp) if i == 4 else (far[2 * (i % 2):2 * (i % 2) + 2], 0, S.dcr)
+        hand(i >= 2, S.hd, cnt, s_out, T.hx, T.hxs, T.lx, T.lxs, [(q, out + CAPP * k, CAPP * place(q, r), CAPP) for k, q in enumerate(to)])
+        if i == 4:
+            q = origin_of(r)
+            for planes, sem in ((False, S.he1), (True, S.he2)):
+                hand(planes, sem, cnt, S.rsp, T.hr, T.hps, T.hb, T.hbs, [(q, 0, ZC + CAPP * pos(q, r), CAPP)])
+            q = late_of(r)[1]
+            hand(True, S.hret, cnt, S.rsp, T.hr, T.hrs, T.hb, T.hbs, [(q, 3 * CAPP, ZC + CAPP * pos(q, r), CAPP)])
+        else:
+            hand(i >= 2, S.hret, cnt, S.rcr, T.hr, T.hrs, T.hb, T.hbs, [(q, CAPP * k, ZC + CAPP * pos(q, r), CAPP) for k, q in enumerate(to)])
         g.wait_ge(S.loc, n[0])
         return
 
     far, near = order(rank)
-    lists = far + [rank] + near
+    lists = far + near[:2] + [rank] + near[2:]
     half, own, rest = CAPP * len(far), CAPP * (N - 1), CAPP * len(near)
-    origin = [q for q in near if order(q)[1][-1] == rank][0]
-
-    def share_of(q, k):
-        i = order(q)[1].index(rank)
-        return len(share(off(q), k)[i]) if i < k else 0
+    origin, late, fifth = origin_of(rank), late_of(rank), handers(rank)[4]
+    two = 2 * CAPP
+    over = 128 - two
+    eng = len(off(rank))
     ahead_in = sum(len(topo.engines(h, core)) for h in handers(origin))
-    list_in = len(off(origin))
-    near_in = sum(2 * share_of(q, 2) for q in near)
-    near_back = sum(share_of(q, 3) + (share_of(q, 2) or share_of(q, 3)) for q in near)
+    near_in, near_back = 2 * eng, 5 * eng
     far_in = sum(2 * len(share(topo.engines(handers(q)[0], core), 2)[0]) for q in far)
     v, sc, te, sy = g.vector, g.scalar, g.tensor, g.sync
     n, nf, nl = [0], [0], [0]
@@ -155,16 +164,16 @@ def rank_program(g, core, T, topo):
     def ts(*a):
         op(v.tensor_scalar(*a))
 
-    def fused(t, *sems):
-        for s in sems:
-            g.wait_ge(s, 1)
+    def fused(t, *waits):
+        for s, k in waits:
+            g.wait_ge(s, k)
         g.remote_dma_fused([send(*a) for a in t], local_sem=S.loc)
         nl[0] += sum(len(a[1]) for a in t)
 
-    def to_far(bc, bp, sem_c, sem_p, sem, dc, dp):
-        for planes in (False, True):
-            fused([(handers(rank)[2 * planes + i], inside(rank, 2 * planes + i), sem, run(planes, bc, bp, 96 * i, 96 * i + 96), run(planes, dc, dp, 0, 96))
-                   for i in range(2)], sem_p if planes else sem_c)
+    def to_far(parts, wait, sem, dc, dp):
+        for i, (bc, bp, a, s) in enumerate(parts):
+            fused([(handers(rank)[i], inside(rank, i), sem, cod(bc, a, a + two), cod(dc, 0, two))], (s, 1))
+        fused([(handers(rank)[2 + i], inside(rank, 2 + i), sem, bp[:, a:a + two], dp[:, 0:two]) for i, (bc, bp, a, s) in enumerate(parts)], wait)
 
     def to_near(to, first, bc, dc, sem):
         t = []
@@ -173,10 +182,13 @@ def rank_program(g, core, T, topo):
             t.append((ranks[q], share(off(rank), len(to))[i], sem, cod(bc, a, a + CAPP), cod(dc, b, b + CAPP)))
         return t
 
+    def zeros(m):
+        return T.rtt[:, 32:32 + m]
+
     sc.dma_start(T.rtt[:, 0:32], T.rt[:, 0:32]).then_inc(S.srt, 16)
     sy.dma_start(T.xt[:, 4 * ZC:4 * ZC + 512], T.x[:]).then_inc(S.sx, 16)
-    sc.dma_start(T.wt[:], T.w[:]).then_inc(S.sw, 16)
-    sy.dma_start(T.ut[:], T.u[:]).then_inc(S.su0, 16)
+    sy.dma_start(T.wt[:], T.w[:]).then_inc(S.sw, 16)
+    sy.dma_start(T.rtt[:, 576:704], T.u[:, 0:128]).then_inc(S.su0, 16)
 
     def iota(out, pattern, base, sem):
         g.iota(out, pattern, base, 0, allow_small_or_imprecise_dtypes=True).then_inc(sem, 1)
@@ -191,303 +203,311 @@ def rank_program(g, core, T, topo):
             iota(out[:, a:a + 2 * m - 1:2], [[step, m]], value(a), sem)
             i, k = i + m, k + 1
         return k
+
+    def first(e):
+        i = lists.index(e)
+        return PLACES * (i // 4 * 2 + i % 2 + 1) + i % 4 // 2
     g.iota(T.ip[:], [[0, 1]], 0, 1).then_inc(S.gi, 1)
-    iota(T.e_[:], [[2, 4]], 0, S.ge1)
-    nk = columns(T.kv, lambda e: DUMP + TOK * lists.index(e) - 1, S.gk)
-    iota(T.kv[:, N:32], [[0, 32 - N]], 0, S.gk)
-    nk += 1
-    iota(T.th[:, 1, :], [[-1, 8]], 1, S.gth)
-    iota(T.th[:, 0, :], [[-1, 8]], 0, S.gth)
+    iota(T.e_[:], [[2, 4]], 32 - N, S.ge1)
+    iota(T.dj[:], [[1, N], [-1, N]], 0, S.gth)
     iota(T.q_[:], [[0, 2], [1, 16]], ZC, S.gq)
+    nk = columns(T.kb, lambda e: first(e) - 2, S.gk)
 
     m = TOK // 4
-    fused([(handers(rank)[k], ahead(rank, k), S.he, cod(T.xq, ZC + m * k, ZC + m * k + m), cod(T.he, 0, m)) for k in range(4)], S.sxq)
-    fused([(handers(rank)[4], ahead(rank, 4), S.he, T.xs[:, ZC:ZC + TOK], T.hes[:, 0:TOK])])
-    iota(T.zst[:, 0:2, :], [[0, 2], [0, 32]], 0, S.gz)
-    iota(T.z[:], [[0, 32]], ZC - DUMP, S.gz)
-    na = columns(T.ka, lambda e: CAPP * pos(rank, e) - TOK * lists.index(e), S.ga)
+    fused([(handers(rank)[k], ahead(rank, k), S.he, cod(T.xq, ZC + m * k, ZC + m * k + m), cod(T.he, 0, m)) for k in range(4)], (S.sxq, 1))
+    fused([(fifth, ahead(rank, 4), S.he, T.xs[:, ZC:ZC + TOK], T.hes[:, 0:TOK])])
+    na = columns(T.ka, lambda e: 2 * (ZC + CAPP * pos(rank, e) + over * (e == rank) - 1), S.ga)
+    iota(T.en[:], [[1, N]], 0, S.ga)
+    na += 1
+    iota(T.zst[:, :, N + 1:32], [[0, 2], [0, 31 - N]], 0, S.gz)
 
-    op(v.memset(T.rtt[:, 32:512], 0.0))
+    op(v.memset(zeros(512), 0.0))
     v.wait_ge(S.gi, 1)
     ts(T.ii[:, 0:1], T.ip[:], 7, None, A.bitwise_and)
     ts(T.ii[:, 1:2], T.ip[:], 3, 1, A.logical_shift_right, A.bitwise_and)
-    fl(v.memset(T.xt[:, 0:4 * ZC], 0.0))
-    fl(v.memset(T.sign[:], 1.0))
+    fl(v.tensor_scalar(T.ii[:, 2:3], T.ip[:], 112, None, A.bitwise_and))
+    fl(v.tensor_scalar(T.ii[:, 3:4], T.ip[:], 15, None, A.bitwise_and))
     done()
     op(v.tensor_copy(T.ff[:, 0:2], T.ii[:, 0:2]))
-    fl(v.tensor_scalar(T.ii[:, 2:3], T.ip[:], 112, None, A.bitwise_and))
-    fl(v.tensor_scalar(T.ii[:, 3:4], T.ip[:], 31, None, A.bitwise_and))
+    v.quantize_mx(T.rp[:, 128:256], T.rps[:, 128:256], zeros(512)).then_inc(S.srz0, 1)
     v.wait_ge(S.ge1, 1)
     done()
-    op(v.tensor_scalar(T.lp[:, 0:4], T.e_[:], T.ff[:, 1:2], T.ff[:, 0:1], A.add, A.max))
-    op(v.tensor_scalar(T.lp[:, 4:8], T.e_[:], T.ff[:, 1:2], T.ff[:, 0:1], A.add, A.min))
+    op(v.tensor_scalar(T.lp[:, 0:4], T.e_[:], 0.0, T.ff[:, 0:1], A.mult, A.add))
+    op(v.tensor_scalar(T.lp[:, 4:8], T.e_[:], T.ff[:, 1:2], None, A.add))
     listed_pairs = n[0]
     fdone()
     v.tensor_copy(T.ff[:, 2:4], T.ii[:, 2:4]).then_inc(S.sff, 1)
-    fl(v.memset(T.sign[:, 0:64:9], -1.0))
+    v.wait_ge(S.gth, 1)
+    fl(v.tensor_scalar(T.thr[:], T.dj[:], 0.0, TINY, A.is_le, A.mult))
 
+    sc.wait_ge(S.v, 1)
+    sc.activation(T.xt[:, 0:4 * ZC], zeros(4 * ZC), F.Copy).then_inc(S.sx0, 1)
+    sc.activation(T.on[:], zeros(128), F.Copy).then_inc(S.sx0, 1)
+    for k in range(1, 5):
+        sc.activation(T.win[:, PLACES * k:PLACES * k + two], zeros(two), F.Copy).then_inc(S.swz, 1)
+    sc.wait_ge(S.sx0, 2)
+    sc.activation(T.on[64:96, 32:64], T.rtt[64:96, 32:64], F.Copy, bias=1.0).then_inc(S.swz, 1)
+    sc.activation(T.on[96:128, 32:96], T.rtt[96:128, 32:96], F.Copy, bias=1.0).then_inc(S.swz, 1)
+
+    sc.wait_ge(S.srt, 16)
+    sc.activation(T.rtt[:, 544:576], T.rtt[:, 0:32], F.Copy, scale=-1.0).then_inc(S.sng, 1)
     v.wait_ge(S.srt, 16)
     done()
-    v.quantize_mx(T.rq[:], T.rs[:], T.rtt[:]).then_inc(S.srq, 1)
-    fdone()
-    fl(v.memset(T.sign[:, 0:64:8], 0.0))
-    v.wait_ge(S.srq, 1)
-    v.tensor_copy(w32(T.rp, 0, 128), w32(T.rq, 0, 128).indirect(T.lp[:])).then_inc(S.srp, 1)
-    sc.wait_ge(S.v, 1)
-    sc.activation(T.win[:, 0:480], T.rtt[:, 32:512], F.Copy).then_inc(S.swz, 1)
-    sc.wait_ge(S.srq, 1)
+    v.quantize_mx(T.rq[:], T.rs[:], T.rtt[:, 0:512]).then_inc(S.srq, 1)
+    v.wait_ge(S.sng, 1)
+    v.quantize_mx(T.rn[:], T.rns[:], T.rtt[:, 64:576]).then_inc(S.srq, 1)
     sc.wait_ge(S.v, listed_pairs)
-    sc.activation(T.rps[:, 0:128], T.rs[:, 0:128].indirect(T.lp[:]), F.Copy).then_inc(S.srps, 1)
-    sc.activation(T.win[:, 480:960], T.rtt[:, 32:512], F.Copy).then_inc(S.swz, 1)
-    sc.activation(T.win[:, 960:1056], T.rtt[:, 32:128], F.Copy).then_inc(S.swz, 1)
+    for k, (q_, s_, a) in enumerate(((T.rq, T.rs, 0), (T.rn, T.rns, 96))):
+        b = 64 - 64 * k
+        if k:
+            v.wait_ge(S.sx0, 2)
+            v.wait_ge(S.sx, 16)
+            v.quantize_mx(T.xq[:], T.xs[:], T.xt[:]).then_inc(S.sxq, 1)
+        v.wait_ge(S.srq, k + 1)
+        v.tensor_copy(w32(T.rp, b, b + 64), w32(q_, a, 128).indirect(T.lp[:, 4 * k:4 * k + 4])).then_inc(S.srp, 1)
+        sc.wait_ge(S.srq, k + 1)
+        sc.activation(T.rps[:, b:b + 64], s_[:, a:128].indirect(T.lp[:, 4 * k:4 * k + 4]), F.Copy).then_inc(S.srps, 1)
     sc.wait_ge(S.sff, 1)
     sc.wait_ge(S.gq, 1)
+    sc.activation(T.sb[:, 2:3], T.ff[:, 3:4], F.Sign, bias=-N - 0.5).then_inc(S.ssb, 1)
     sc.activation(T.vals[:], T.q_[:], F.Identity, bias=T.ff[:, 2:3]).then_inc(S.scn, 1)
-    sc.wait_ge(S.gk, nk)
-    sc.activation(T.kt[:], T.kv[:, 0:8], F.Copy, bias=1.0 * CAPP).then_inc(S.scn, 1)
-    sc.activation(T.cw[:, 0:1], T.ff[:, 3:4], F.Copy, bias=0.5).then_inc(S.scw, 1)
-    sc.activation(T.cr[:], T.ff[:, 3:4], F.Relu, scale=100.0, bias=-100.0 * (N - 2)).then_inc(S.scw, 1)
-    sc.wait_ge(S.scw, 2)
-    sc.activation(T.cw[:, 2:3], T.cr[:], F.Copy, scale=-1.0).then_inc(S.scw, 1)
-    v.wait_ge(S.sx, 16)
-    v.quantize_mx(T.xq[:], T.xs[:], T.xt[:]).then_inc(S.sxq, 1)
-    te.wait_ge(S.srp, 1)
-    te.wait_ge(S.srps, 1)
+    te.wait_ge(S.srz0, 1)
     te.wait_ge(S.sxq, 1)
-    te.matmul_mx(T.psb[:, 0:128], T.xq[:, ZC:ZC + TOK], T.xs[:, ZC:ZC + TOK], T.rp[:, 0:128], T.rps[:, 0:128], True, True).then_inc(S.mS, 1)
-    op(v.memset(T.nn[:], 0.0))
-    v.wait_ge(S.gk, nk)
-    op(v.transpose(T.kvt[:], T.kv[:]))
-    op(v.memset(T.lo[:], 0))
+    for k in range(2):
+        b = 64 - 64 * k
+        te.wait_ge(S.srp, k + 1)
+        te.wait_ge(S.srps, k + 1)
+        c = te.matmul_mx(T.psb[:, 0:128], T.xq[:, ZC:ZC + TOK], T.xs[:, ZC:ZC + TOK], T.rp[:, b:b + 128], T.rps[:, b:b + 128], k == 0, k == 1)
+    c.then_inc(S.mS, 1)
+    fl(v.memset(T.nn[:], 0.0))
+    fl(v.memset(T.lo[:], 0))
 
     v.wait_ge(S.mS, 1)
-    op(v.tensor_copy(T.bs[:], T.psb[:, 64:128]))
-    done()
-    tt(T.gt[:], T.psb[:, 0:64], T.bs[:], A.is_gt)
     fdone()
+    tt(T.gt[:], T.psb[:, 0:64], T.thr[:], A.is_ge)
     done()
-    op(v.tensor_tensor_scan(T.rk[:], T.sign[:], T.gt[:], 0.0, A.mult, A.add))
-    v.wait_ge(S.gth, 2)
+    op(v.tensor_reduce(T.cnt[:], T.gt[:], X, A.add))
+    counted = n[0]
     done()
-    for d, b, p, c in ((64, 0, 64, 0), (32, 0, 32, 0), (64, 32, 32, 32), (96, 0, 32, 32), (96, 64, 32, 64), (0, 0, 128, 96)):
-        tt(T.nn[d:d + p, c:c + 8], T.rk[b:b + p, 7:64:8], T.th[b:b + p, 1, :], A.is_le)
-    for k in range(2):
-        fl(v.tensor_tensor(T.oh2[:, k, :], T.rk[:, 7:64:8], T.th[:, k, :], A.is_equal))
+    for d, b, p, c in ((64, 0, 64, 0), (32, 0, 32, 0), (0, 0, 128, 96)):
+        ts(T.nn[d:d + p, c:c + 8], T.cnt[b:b + p, :], 1.5, 2.0, A.is_le, A.mult)
+    sc.wait_ge(S.v, counted)
+    sc.wait_ge(S.f, nf[0])
+    for d, b, p, c in ((64, 32, 32, 32), (96, 0, 32, 32), (96, 64, 32, 64)):
+        sc.activation(T.nn[d:d + p, c:c + 8], T.cnt[b:b + p, :], F.Sign, scale=-1.0, bias=1.5).then_inc(S.snn, 1)
+    sc.wait_ge(S.ssb, 1)
+    sc.activation(T.sb[:, 0:1], T.sb[:, 2:3], F.Copy, scale=-0.25, bias=0.75).then_inc(S.ssb, 1)
+    sc.activation(T.sb[:, 1:2], T.sb[:, 2:3], F.Copy, scale=-0.5 * MID, bias=-0.5 * MID).then_inc(S.ssb, 1)
+    fl(v.tensor_scalar(T.oh2[:, 0, :], T.cnt[:], 0.0, None, A.is_equal))
+    v.wait_ge(S.snn, 3)
     done()
     op(v.transpose(T.nt[:], T.nn[:]))
+    fl(v.tensor_scalar(T.oh2[:, 1, :], T.cnt[:], 1.0, None, A.is_equal))
+    v.wait_ge(S.swz, 6)
     done()
-    op(v.tensor_tensor_scan(T.cs[:], T.nt[:], T.nt[:], T.kvt[:, 0:1], A.add, A.max))
+    op(v.tensor_tensor_scan(T.cs[:], T.nt[:], T.on[:], 0.0, A.add, A.add))
+    v.wait_ge(S.f, nf[0] - 1)
+    v.wait_ge(S.gk, nk)
+    fl(v.tensor_tensor(T.mk[:, 0, :], T.oh2[:, 0, :], T.kb[:], A.mult))
     done()
     op(v.transpose(T.ct[:], T.cs[:, 96:128]))
-    fdone()
+    v.wait_ge(S.f, nf[0] - 1)
+    fl(v.tensor_tensor(T.mk[:, 1, :], T.oh2[:, 1, :], T.kb[:], A.mult))
     done()
-    for k in range(2):
-        tt(T.pr[:, k, :], T.oh2[:, k, :], T.ct[:, 0:8], A.mult)
+    tt(T.pr[:, 0, :], T.mk[:, 0, :], T.ct[:, 0:8], A.add)
+    fdone()
+    tt(T.pr[:, 1, :], T.mk[:, 1, :], T.ct[:, 0:8], A.add)
+    fl(v.tensor_tensor(T.sd[:], T.oh2[:, 1, :], T.oh2[:, 0, :], A.subtract))
     done()
     op(v.tensor_reduce(T.of[:], T.pr[:], X, A.max))
-    v.wait_ge(S.scn, 2)
-    fl(v.tensor_tensor(T.un[:], T.ct[:, 0:8], T.kt[:], A.is_le))
-    v.wait_ge(S.swz, 3)
+    fl(v.tensor_scalar(T.nu[:], T.ct[:, 0:8], 2.0 * CAPP, 2.0, A.is_gt, A.mult))
+    v.wait_ge(S.scn, 1)
     done()
     op(v.tensor_copy(T.win[:].indirect(T.of[:]), T.vals[:]))
+    scattered = n[0]
+    fl(v.tensor_scalar(T.un[:], T.ct[:, 0:8], 2.0 * CAPP, None, A.is_le))
+    done()
+
+    def lay(k, d):
+        return T.dd[:, 3 * k:3 * k + 3, d, :, :], T.win[:, PLACES * (k + 1):PLACES * (k + 1) + two]
+
+    def turn(h, j):
+        return v.transpose(T.ot[:, 384 * h + 192 * j:384 * h + 192 * j + 192], T.dd[:, 6 * h:6 * h + 6, :, :, j])
+    sc.wait_ge(S.v, scattered)
+    sc.activation(*lay(0, 1), F.Copy).then_inc(S.sdd, 1)
+    for k, d in ((2, 0), (2, 1), (3, 0)):
+        sc.activation(*lay(k, d), F.Copy).then_inc(S.sde, 1)
+    for k, d in ((0, 0), (1, 0), (1, 1)):
+        op(v.tensor_copy(*lay(k, d)))
+    fl(v.tensor_scalar(T.ub[:], T.ct[:, 0:8], 2.0 * CAPP, BIG, A.is_le, A.mult))
+    v.wait_ge(S.sdd, 1)
+    done()
+    op(turn(0, 0))
+    op(turn(0, 1))
+    fl(v.tensor_copy(*lay(3, 1)))
+    done()
+    tt(T.ta[:, 0:12], T.ot[:, 0:384:32], T.ot[:, 16:384:32], A.add)
+    v.wait_ge(S.sde, 3)
+    fdone()
+    fl(turn(1, 0))
+    done()
+    tt(T.tb[0:64, 0:12], T.ta[0:64, 0:12], T.ta[64:128, 0:12], A.add)
+    fl(turn(1, 1))
+    done()
+    for p in (0, 32, 64, 96):
+        tt(T.od[p:p + 32, 0:12], T.tb[0:32, 0:12], T.tb[32:64, 0:12], A.add)
+    far_list = n[0]
+    fdone()
+    fl(v.tensor_tensor(T.ta[:, 12:24], T.ot[:, 384:768:32], T.ot[:, 400:768:32], A.add))
+
+    def picked(lo, hi, s1, s2):
+        a, b = 16 * lo, 16 * hi
+        v.tensor_copy(w32(T.xg, a, b), w32(T.xq, 0, ZC + TOK).indirect(T.od[:, lo:hi])).then_inc(s1, 1)
+        sc.activation(T.xgs[:, a:b], T.xs[:, 0:ZC + TOK].indirect(T.od[:, lo:hi]), F.Copy).then_inc(s2, 1)
+    done()
+    sc.wait_ge(S.sxq, 1)
+    sc.wait_ge(S.v, far_list)
+    picked(0, 6, S.sg0, S.sg1s)
+    picked(6, 12, S.sg1, S.sg1s)
+    fdone()
+    tt(T.tb[0:64, 12:24], T.ta[0:64, 12:24], T.ta[64:128, 12:24], A.add)
+    done()
+    for p in (0, 32, 64, 96):
+        tt(T.od[p:p + 32, 12:24], T.tb[0:32, 12:24], T.tb[32:64, 12:24], A.add)
+    near_list = n[0]
     v.wait_ge(S.ga, na)
     fl(v.tensor_tensor(T.c3_[:], T.ct[:, 0:8], T.ka[:], A.add))
     done()
-    scattered = n[0]
-
-    def lay(i, d):
-        return T.dd[:, i, :, d, :], T.win[:, DUMP + TOK * i:DUMP + TOK * i + CAPP]
-    sc.wait_ge(S.v, scattered)
-    for i in range(8):
-        if i != 3:
-            sc.activation(*lay(i, 1), F.Copy).then_inc(S.sde if i > 3 else S.sdd, 1)
-    for i in range(4):
-        op(v.tensor_copy(*lay(i, 0)))
-    op(v.tensor_copy(*lay(3, 1)))
-    fl(v.tensor_copy(*lay(4, 0)))
-    v.wait_ge(S.sdd, 3)
-    done()
-    op(v.transpose(T.ot[:, 0:384], T.dd[:, 0:4]))
-    fl(v.tensor_copy(*lay(5, 0)))
-    fl(v.tensor_copy(*lay(6, 0)))
-    done()
-    tt(T.ta[:, 0:12], T.ot[:, 0:384:32], T.ot[:, 16:384:32], A.add)
-    fl(v.tensor_copy(*lay(7, 0)))
-    done()
-    tt(T.tb[0:64, 0:12], T.ta[0:64, 0:12], T.ta[64:128, 0:12], A.add)
-    v.wait_ge(S.sde, 4)
-    fdone()
-    done()
-    for p in (0, 32):
-        tt(T.od[p:p + 32, 0:12], T.tb[0:32, 0:12], T.tb[32:64, 0:12], A.add)
-    done()
-    far_list = n[0]
-    v.tensor_copy(T.od[64:128, 0:12], T.od[0:64, 0:12]).then_inc(S.sod1, 1)
-    fl(v.transpose(T.ot[:, 384:768], T.dd[:, 4:8]))
-
-    def picked(lo, hi, a, s1, s2):
-        b = a + 16 * (hi - lo)
-        v.tensor_copy(w32(T.xg, a, b), w32(T.xq, 0, ZC + TOK).indirect(T.od[:, lo:hi])).then_inc(s1, 1)
-        sc.activation(T.xgs[:, a:b], T.xs[:, 0:ZC + TOK].indirect(T.od[:, lo:hi]), F.Copy).then_inc(s2, 1)
-    v.wait_ge(S.sod1, 1)
-    sc.wait_ge(S.sod1, 1)
-    sc.wait_ge(S.v, far_list)
-    picked(0, 12, 0, S.sg1, S.sg1s)
-    fdone()
-    tt(T.ta[:, 12:24], T.ot[:, 384:768:32], T.ot[:, 400:768:32], A.add)
-    fl(v.tensor_tensor(T.c2_[:], T.un[:], T.c3_[:], A.mult))
-    done()
-    tt(T.tb[0:64, 12:24], T.ta[0:64, 12:24], T.ta[64:128, 12:24], A.add)
-    done()
-    for p in (0, 32):
-        tt(T.od[p:p + 32, 12:24], T.tb[0:32, 12:24], T.tb[32:64, 12:24], A.add)
-    done()
-    near_list = n[0]
-    v.tensor_copy(T.od[64:128, 12:24], T.od[0:64, 12:24]).then_inc(S.sod2, 1)
-    v.wait_ge(S.sod2, 1)
-    sc.wait_ge(S.sod2, 1)
+    sc.activation(T.xes[:, 0:ZC], T.xs[:, 0:ZC + TOK].indirect(T.lo[:, 0:1]), F.Copy).then_inc(S.sz, 1)
     sc.wait_ge(S.v, near_list)
-    picked(12, 21, half, S.sg2, S.sg2s)
+    picked(12, 21, S.sg2, S.sg2s)
+    fdone()
+    fl(v.tensor_tensor(T.c2_[:], T.un[:], T.c3_[:], A.mult))
+    fl(v.tensor_copy(w32(T.xe, 0, ZC), w32(T.xq, 0, ZC + TOK).indirect(T.lo[:, 0:1])))
 
-    to_far(T.xg, T.xgs, S.sg1, S.sg1s, S.hd, T.hx, T.hxs)
-    g.wait_ge(S.sod2, 1)
-    g.wait_ge(S.v, near_list)
-    fused([(ranks[near[2]], off(rank), S.dl, T.od[:, 21:24], T.le[:, 0:3])])
-    fused(to_near([(q, CAPP * place(q, rank)) for q in near[:2]], half + CAPP, T.xg, T.lx, S.dsp)
-          + [(handers(rank)[4], inside(rank, 4), S.hd, T.xgs[:, half - CAPP:half + 3 * CAPP], T.hxs[:, 0:4 * CAPP])], S.sg2, S.sg2s)
-    iota(T.jr[:], [[1, 128]], ZC, S.gh)
-    iota(T.jra[:], [[1, 128]], ZC + TOK, S.gh)
-    iota(T.wa[:], [[0, 32]], 0, S.gh)
+    to_far([(T.xg, T.xgs, 0, S.sg0), (T.xg, T.xgs, two, S.sg1)], (S.sg1s, 2), S.hd, T.hx, T.hxs)
+    fused([(ranks[near[2]], off(rank), S.dl, T.od[:, 21:24], T.le[:, 0:3])], (S.v, near_list))
+    fused(to_near([(q, CAPP * place(q, rank)) for q in near[:2]], half, T.xg, T.lx, S.dsp)
+          + [(fifth, inside(rank, 4), S.hd, T.xgs[:, half - CAPP:half + 3 * CAPP], T.hxs[:, 0:4 * CAPP])], (S.sg2, 1), (S.sg2s, 1))
+    iota(T.j0[:], [[16, 8], [0, 8]], ZC, S.gh)
+    iota(T.vz[:, :, N:N + 1], [[0, 8]], 0, S.gh)
+    iota(T.wr[:, 0:ZC], [[0, ZC]], -100, S.gh)
 
     v.wait_ge(S.sw, 16)
     for i in range(4):
         v.quantize_mx(T.wq[:, 128 * i:128 * i + 128], T.ws[:, 128 * i:128 * i + 128], T.wt[:, 512 * i:512 * i + 512]).then_inc(S.swq, 1)
+    sy.wait_ge(S.swq, 4)
+    sy.dma_start(T.vt[:], T.v[:]).then_inc(S.sv0, 16)
 
-    te.wait_ge(S.sg2, 1)
-    te.wait_ge(S.sg2s, 1)
-    for i in range(4):
-        te.wait_ge(S.swq, i + 1)
-        te.matmul_mx(T.psa[:, 512 * i:512 * i + 128], T.wq[:, 128 * i:128 * i + 128], T.ws[:, 128 * i:128 * i + 128],
-                     T.xg[:, half:half + 128], T.xgs[:, half:half + 128], True, True).then_inc(S.mo, 1)
-    for i in range(4):
-        sc.wait_ge(S.mo, i + 1)
-        sc.activation(T.hto[:, i:512:4], T.psa[:, 512 * i:512 * i + 128], F.Relu, scale=0.0625).then_inc(S.sro, 1)
-
+    a = half + rest
     fdone()
-    for k in range(2):
-        tt(T.ph[:, k, :], T.oh2[:, k, :], T.c2_[:], A.mult)
-    v.wait_ge(S.gz, 2)
-    for k in range(2):
-        fl(v.tensor_tensor(T.zst[:, k, 0:8], T.oh2[:, k, :], T.un[:], A.mult))
-    done()
-    op(v.tensor_reduce(T.vm[:], T.ph[:], X, A.max))
-    done()
-    ts(T.tk[:], T.vm[:], 0.0, BIG, A.is_gt, A.mult)
-    for k in range(2):
-        fl(v.tensor_scalar(T.zst[:, 3 + k, :], T.z[:], T.vm[:, k:k + 1], 0.0, A.add, A.max))
-    done()
-    tt(T.mm[:, 0:1], T.tk[:, 1:2], T.tk[:, 0:1], A.subtract)
-    done()
-    ts(T.zst[:, 2, :], T.z[:], 0.0, T.mm[:, 0:1], A.mult, A.add)
-    fdone()
-    done()
-    op(v.transpose(T.zt[:], T.zst[:]))
-    sc.wait_ge(S.v, n[0])
-    for b in range(4):
-        sc.activation(T.rz[0:32, :, 32 * b:32 * b + 32], T.zt[32 * b:32 * b + 32, :, :], F.Copy).then_inc(S.srz, 1)
-    sy.wait_ge(S.srz, 4)
-    for b in range(1, 4):
-        sy.dma_start(T.rz[32 * b:32 * b + 32, :, :], T.rz[0:32, :, :]).then_inc(S.srd, 16)
-
-    a = CAPP * place(rank, origin)
-    op(v.tensor_copy(w32(T.xe, 0, ZC), w32(T.xq, 0, ZC + TOK).indirect(T.lo[:, 0:1])))
-    sc.activation(T.xes[:, 0:ZC], T.xs[:, 0:ZC + TOK].indirect(T.lo[:, 0:1]), F.Copy).then_inc(S.sz, 1)
-    v.wait_ge(S.sro, 4)
-    v.quantize_mx(T.hb[:, ZC + own:ZC + own + 128], T.hbs[:, ZC + own:ZC + own + 128], T.hto[:]).then_inc(S.so, 1)
-    done()
     sc.wait_ge(S.sz, 1)
     for q in (v, sc):
         q.wait_ge(S.de, ahead_in)
-        q.wait_ge(S.dl, list_in)
-    v.tensor_copy(w32(T.lx, a, a + CAPP), w32(T.xe, 0, ZC + TOK).indirect(T.le[:, 0:3])).then_inc(S.sep, 1)
-    sc.activation(T.lxs[:, a:a + CAPP], T.xes[:, 0:ZC + TOK].indirect(T.le[:, 0:3]), F.Copy).then_inc(S.seps, 1)
+        q.wait_ge(S.dl, eng)
+    v.tensor_copy(w32(T.xg, a, a + CAPP), w32(T.xe, 0, ZC + TOK).indirect(T.le[:, 0:3])).then_inc(S.sep, 1)
+    sc.activation(T.xgs[:, a:a + CAPP], T.xes[:, 0:ZC + TOK].indirect(T.le[:, 0:3]), F.Copy).then_inc(S.seps, 1)
 
-    def expert(h):
-        a, m = (0, half) if h else (half, rest)
-        ps, t0, rs = (T.psb, 0, S.r2s) if h else (T.psa, 4 * half, S.r1s)
-        if h:
-            te.wait_ge(S.dcr, far_in)
-        else:
-            te.wait_ge(S.sro, 4)
-            te.wait_ge(S.dsp, near_in)
-            te.wait_ge(S.sep, 1)
-            te.wait_ge(S.seps, 1)
+    tt(T.ph[:, 3, :], T.sd[:], T.ub[:], A.mult)
+    tt(T.ph[:, 4, :], T.oh2[:, 0, :], T.en[:], A.mult)
+    termed = n[0]
+    tt(T.ph[:, 0, :], T.oh2[:, 1, :], T.en[:], A.mult)
+    for k in range(2):
+        tt(T.ph[:, 1 + k, :], T.oh2[:, k, :], T.c2_[:], A.mult)
+    v.wait_ge(S.v, termed)
+    fl(v.tensor_reduce(T.zst[:, 1, N - 1:N + 1], T.ph[:, 3:5, :], X, A.add))
+    tt(T.zst[:, 0, 0:N], T.cnt[:], T.nu[:], A.add)
+    v.wait_ge(S.gz, 1)
+    v.wait_ge(S.v, n[0] - 1)
+    op(v.tensor_reduce(T.zst[:, 0, N:N + 3], T.ph[:, 0:3, :], X, A.add))
+    fdone()
+    ts(T.zst[:, 1, 0:N - 1], zeros(N - 1), T.zst[:, 1, N - 1:N], None, A.add)
+
+    def expert(h, waits, ps, xc, xp, a, m, skip, tile, t0, vecs, rs, outs):
+        for s, k in waits:
+            te.wait_ge(s, k)
         for i in range(4):
             te.matmul_mx(ps[:, 512 * i:512 * i + m], T.wq[:, 128 * i:128 * i + 128], T.ws[:, 128 * i:128 * i + 128],
-                         T.lx[:, a:a + m], T.lxs[:, a:a + m], True, True).then_inc(S["m%d" % (4 * h + i)], 1)
+                         xc[:, a:a + m], xp[:, a:a + m], True, True).then_inc(S["m%d" % (4 * h + i)], 1)
         for i in range(4):
-            src, dst = ps[:, 512 * i:512 * i + m], T.ht[:, t0 + i:t0 + 4 * m:4]
-            vec = i == 3 or h and i == 1
-            q = v if vec else sc
+            src, dst = ps[:, 512 * i + skip:512 * i + m], tile[:, 4 * (t0 + skip) + i:4 * (t0 + m):4]
+            q = v if i in vecs else sc
             q.wait_ge(S["m%d" % (4 * h + i)], 1)
-            if vec:
+            if i in vecs:
                 ts(dst, src, 0.0, 0.0625, A.max, A.mult)
             else:
                 sc.activation(dst, src, F.Relu, scale=0.0625).then_inc(rs, 1)
-        v.wait_ge(rs, 2 if h else 3)
+        v.wait_ge(rs, 4 - len(vecs))
         done()
-        v.quantize_mx(T.hq[:, a:a + m], T.hqs[:, a:a + m], T.ht[:, t0:t0 + 4 * m]).then_inc(S.q2 if h else S.q1, 1)
+        for oc, os_, b, sem in outs:
+            v.quantize_mx(oc, os_, tile[:, 4 * b:4 * b + 512]).then_inc(sem, 1)
 
-    expert(1)
-    to_far(T.hq, T.hqs, S.q2, S.q2, S.hret, T.hr, T.hrs)
-    expert(0)
-    fused(to_near([(q, ZC + CAPP * pos(q, rank)) for q in near], half, T.hq, T.hb, S.rsp)
-          + [(handers(rank)[4], inside(rank, 4), S.hret, T.hqs[:, half - CAPP:half + rest], T.hrs[:, 0:half])], S.q1)
-    a, b = half + 2 * CAPP, ZC + CAPP * pos(near[2], rank)
-    fused([(ranks[near[2]], share(off(rank), 3)[2], S.rsp, T.hqs[:, a:a + CAPP], T.hbs[:, b:b + CAPP])])
-    sy.wait_ge(S.dsp, near_in)
-    sy.dma_start(T.vt[:], T.v[:]).then_inc(S.sv0, 16)
+    expert(2, ((S.sg2, 1), (S.sg2s, 1), (S.swq, 4), (S.sep, 1), (S.seps, 1)), T.psa, T.xg, T.xgs, a + CAPP - 128, 128, 0, T.hto, 0,
+           (3,), S.sro, [(T.ho[:], T.hos[:], 0, S.so1)])
+    op(v.transpose(T.zt[:], T.zst[:]))
+    turned = n[0]
+    a = 128 - CAPP
+    fused([(fifth, inside(rank, 4), S.he1, cod(T.ho, a, 128), cod(T.hr, 0, CAPP))], (S.so1, 1))
+    fused([(fifth, inside(rank, 4), S.he2, T.hos[:, a:128], T.hps[:, 0:CAPP])])
+    a = half - 128
+    expert(1, ((S.dcr, far_in),), T.psb, T.lx, T.lxs, 0, half, 0, T.ht, 0, (1, 3), S.r2s,
+           [(T.hp[:], T.hpp[:], 0, S.q3), (T.hq[:, a:half], T.hqs[:, a:half], a, S.q2)])
+    to_far([(T.hp, T.hpp, 0, S.q3), (T.hq, T.hqs, two, S.q2)], (S.q2, 1), S.hret, T.hr, T.hrs)
+    expert(0, ((S.so1, 1), (S.dsp, near_in)), T.psa, T.lx, T.lxs, half - over, 128, over, T.ht, half - over, (3,), S.r1s,
+           [(T.hq[:, half:half + 128], T.hqs[:, half:half + 128], half - over, S.q1)])
+    back = [(q, ZC + CAPP * pos(q, rank)) for q in late]
+    a, b = half + over, back[0][1]
+    fused(to_near(back, a, T.hq, T.hb, S.rsp) + [(fifth, inside(rank, 4), S.hret, T.hqs[:, a - two:a + two], T.hrs[:, 0:4 * CAPP])], (S.q1, 1))
+    fused([(ranks[late[0]], off(rank), S.rsp, T.hqs[:, a:a + CAPP], T.hbs[:, b:b + CAPP])])
 
+    sc.wait_ge(S.v, turned)
+    sc.wait_ge(S.ssb, 3)
+    for b in range(4):
+        sc.activation(T.rz[0:32, :, 32 * b:32 * b + 32], T.zt[32 * b:32 * b + 32, :, :], F.Identity, scale=T.sb[0:32, 0:1], bias=T.sb[0:32, 1:2]).then_inc(S.srz, 1)
+    v.wait_ge(S.srz, 4)
+    op(v.tensor_copy(T.rz[32:64], T.rz[0:32]))
+    v.quantize_mx(T.hb[:, ZC + own:ZC + own + 128], T.hbs[:, ZC + own:ZC + own + 128], T.hto[:]).then_inc(S.so, 1)
+    done()
+    v.tensor_copy(T.rz[64:128], T.rz[0:64]).then_inc(S.srd, 1)
     v.wait_ge(S.su0, 16)
-    v.quantize_mx(T.uq[:], T.us[:], T.ut[:]).then_inc(S.suq, 1)
+    v.quantize_mx(T.uq[:], T.us[:], T.rtt[:, 192:704]).then_inc(S.suq, 1)
     for q_, s_ in ((T.hb, T.hbs), (T.hab, T.habs)):
         op(v.tensor_copy(w32(q_, 0, ZC), w32(T.xq, 0, ZC + TOK).indirect(T.lo[:, 0:1])))
         sc.activation(s_[:, 0:ZC], T.xs[:, 0:ZC + TOK].indirect(T.lo[:, 0:1]), F.Copy).then_inc(S.sz2, 1)
     v.wait_ge(S.suq, 1)
-    v.tensor_copy(w32(T.up, 0, 128), w32(T.uq, 0, 128).indirect(T.lo[:])).then_inc(S.sup, 1)
-    sc.wait_ge(S.srz, 4)
-    sc.wait_ge(S.srd, 48)
-    for k in range(2):
-        for d in range(2):
-            sc.activation(T.d2[:, k, :, d, :], T.rz[:, 3 + k, :], F.Copy).then_inc(S.sd2, 1)
+    v.tensor_copy(w32(T.up, 0, 128), w32(T.uq, 96, 128).indirect(T.lo[:])).then_inc(S.sup, 1)
+    sc.wait_ge(S.gh, 3)
+    sc.activation(T.jw[:], T.j0[:], F.Identity, bias=T.ff[:, 3:4]).then_inc(S.sjw, 1)
+    sc.wait_ge(S.srd, 1)
+    for d in range(2):
+        sc.activation(T.d2[:, :, d, :], T.rz[:, 0, :], F.Copy).then_inc(S.sd2, 1)
     sc.wait_ge(S.suq, 1)
-    sc.activation(T.ups[:, 0:128], T.us[:, 0:128].indirect(T.lo[:]), F.Copy).then_inc(S.sups, 1)
-    sc.activation(T.ra[:], T.rz[:, 0, :], F.Copy, scale=-6.0, bias=7.0).then_inc(S.ska, 1)
-    sc.activation(T.rb[:], T.rz[:, 1, :], F.Copy, scale=-7.0).then_inc(S.ska, 1)
-    v.wait_ge(S.srz, 4)
-    v.wait_ge(S.srd, 48)
-    v.wait_ge(S.gh, 3)
-    tt(T.pa[:], T.rz[:, 0, :], T.jr[:], A.mult)
-    tt(T.pb[:], T.rz[:, 1, :], T.jra[:], A.mult)
-    v.wait_ge(S.sd2, 4)
+    sc.activation(T.ups[:, 0:128], T.us[:, 96:128].indirect(T.lo[:]), F.Copy).then_inc(S.sups, 1)
+    v.wait_ge(S.sd2, 2)
     op(v.transpose(T.dt[:], T.d2[:]))
-    done()
-    tt(T.pp[:, :, 0, :], T.pa[:], T.pb[:], A.add)
-    sc.wait_ge(S.v, n[0])
-    sc.activation(T.pp[:, :, 1, :], T.pp[:, :, 0, :], F.Copy).then_inc(S.sp1, 1)
-    v.tensor_copy(T.oh[:], T.dt[:, 0:512:32]).then_inc(S.soh, 1)
     v.wait_ge(S.sv0, 16)
     v.quantize_mx(T.vq[:], T.vs[:], T.vt[:]).then_inc(S.svq, 1)
-    v.wait_ge(S.ska, 2)
-    tt(T.kk[:], T.ra[:], T.rb[:], A.add)
-    v.wait_ge(S.sp1, 1)
     done()
-    op(v.transpose(T.ppt[:], T.pp[:]))
+    ts(T.wp[:], T.dt[:, :, 0:N], 1.0 * TOK, None, A.mult)
+    for k in range(2):
+        v.tensor_scalar(T.oh[:, 8 * k:8 * k + 8], T.dt[:, :, N + 1 + k], 1.0 * MID, None, A.add).then_inc(S.soh, 1)
+    v.wait_ge(S.sjw, 1)
+    v.wait_ge(S.gh, 3)
+    done()
+    tt(T.ppt[:], T.wp[:], T.jw[:], A.add)
+    for a in range(ZC + 2 * TOK, ALL, 128):
+        v.quantize_mx(T.hab[:, a:a + 128], T.habs[:, a:a + 128], zeros(512)).then_inc(S.sz3, 1)
+    sc.activation(T.ya[:, ZC + 2 * TOK:ALL], zeros(OUT), F.Copy).then_inc(S.swr, 1)
+    for k in range(2):
+        a = ZC + TOK * k
+        sc.activation(T.wr[:, a:a + TOK], T.rz[:, 1 - k, :], F.Copy).then_inc(S.swr, 1)
+        sc.activation(T.wr[:, a + OUT:a + OUT + TOK], T.rz[:, 1 - k, :], F.Copy, scale=-1.0, bias=-1.0).then_inc(S.swr, 1)
     done()
 
     for q in (v, sc):
-        q.wait_ge(S.soh, 1)
+        q.wait_ge(S.soh, 2)
         q.wait_ge(S.so, 1)
+        q.wait_ge(S.sz3, 2)
         q.wait_ge(S.rsp, near_back)
         q.wait_ge(S.rcr, far_in)
     sc.wait_ge(S.sz2, 2)
@@ -503,54 +523,42 @@ def rank_program(g, core, T, topo):
     te.matmul_mx(T.psa[:, 512:640], T.up[:, 0:128], T.ups[:, 0:128], T.hab[:, ZC:ZC + TOK], T.habs[:, ZC:ZC + TOK], True, True).then_inc(S.mqa, 1)
     te.matmul_mx(T.psa[:, 1024:1296], T.vq[:, 0:128], T.vs[:, 0:128], T.hab[:, 0:272], T.habs[:, 0:272], True, True).then_inc(S.my, 1)
     v.wait_ge(S.mqb, 1)
-    tt(T.qb[:], T.psa[:, 0:128], T.rz[:, 2, :], A.add)
+    tt(T.qb[:], T.psa[:, 0:128], T.rz[:, 1, :], A.add)
     v.wait_ge(S.mqa, 1)
     done()
-    tt(T.ge[:], T.psa[:, 512:640], T.qb[:], A.is_ge)
+    tt(T.ge[:], T.psa[:, 512:640], T.qb[:], A.is_lt)
     done()
-    v.tensor_tensor(T.ww[:], T.ge[:], T.kk[:], A.is_equal).then_inc(S.sww, 1)
+    v.tensor_tensor(T.ww[:], T.ge[:], T.rz[:, 0, :], A.is_equal).then_inc(S.sww, 1)
     v.wait_ge(S.sww, 1)
     v.tensor_tensor_scan(T.cc[:], T.ww[:], T.ww[:], 0.0, A.add, A.max).then_inc(S.scc, 1)
-    for d in range(2):
-        fl(v.tensor_copy(T.vv[:, :, d, :], T.ww[:]))
+    fl(v.tensor_scalar(T.vv[:, :, 0, :], T.ww[:], 1.0, LOST, A.subtract, A.mult))
+    sc.wait_ge(S.my, 1)
+    sc.activation(T.ya[:, 0:ZC + 2 * TOK], T.psa[:, 1024:1296], F.Copy).then_inc(S.sya, 1)
+    sc.wait_ge(S.sww, 1)
+    sc.activation(T.vv[:, :, 1, :], T.ww[:], F.Copy, scale=LOST, bias=-LOST).then_inc(S.svv, 1)
     v.wait_ge(S.scc, 1)
     for d in range(2):
-        ts(T.lv[:, :, d, :], T.cc[:], 1.0 * CAPR, None, A.is_le)
+        ts(T.lv[:, :, d, :], T.cc[:], 1.0 * CAPR, 1.0 * OUT, A.is_gt, A.mult)
     fdone()
+    v.wait_ge(S.svv, 1)
     fl(v.transpose(T.vvt[:], T.vv[:]))
     done()
     op(v.transpose(T.lvt[:], T.lv[:]))
     fdone()
-    fl(v.tensor_tensor(T.wp[:], T.vvt[:, :, 0:8], T.ppt[:, :, 0:8], A.mult))
-    v.wait_ge(S.sgg, 2)
-    op(v.transpose(T.ght[:], T.gh[:]))
+    fl(v.tensor_tensor(T.wp[:], T.vvt[:, :, 0:8], T.ppt[:], A.add))
     fdone()
     done()
-    fl(v.tensor_tensor(T.vz[:], T.wp[:], T.lvt[:, :, 0:8], A.mult))
-    v.wait_ge(S.sgs, 1)
-    op(v.transpose(T.gst[:], T.gs[:]))
-    fdone()
+    tt(T.vz[:, :, 0:8], T.wp[:], T.lvt[:, :, 0:8], A.add)
+    done()
     v.tensor_reduce(T.oz[:], T.vz[:], X, A.max).then_inc(S.soz, 1)
-    done()
-    tt(T.ght[:, :, 0, 8:16], T.ght[:, :, 1, 0:8], T.gst[:, :, 0:8], A.mult)
-    sc.wait_ge(S.my, 1)
-    sc.activation(T.ya[:], T.psa[:, 1024:1296], F.Copy).then_inc(S.sya, 1)
-    sc.wait_ge(S.scw, 3)
-    sc.wait_ge(S.sww, 1)
-    sc.activation(T.gh[:, :, 0, :], T.ww[:], F.Identity, scale=99.5, bias=T.cw[:, 2:3]).then_inc(S.sgg, 1)
-    sc.activation(T.gh[:, :, 1, :], T.ww[:], F.Copy, scale=T.cw[:, 0:1]).then_inc(S.sgg, 1)
-    sc.wait_ge(S.scc, 1)
-    sc.activation(T.gs[:], T.cc[:], F.Sign, scale=-1.0, bias=CAPR + 0.5).then_inc(S.sgs, 1)
     v.wait_ge(S.soz, 1)
-    v.tensor_copy(w32(T.zq, 0, 128), w32(T.hab, 0, 272).indirect(T.oz[:])).then_inc(S.szq, 1)
-    v.tensor_copy(T.zs[:, 0:128], T.habs[:, 0:272].indirect(T.oz[:])).then_inc(S.szs, 1)
+    v.tensor_copy(w32(T.zq, 0, 128), w32(T.hab, 0, ALL).indirect(T.oz[:])).then_inc(S.szq, 1)
+    v.tensor_copy(T.zs[:, 0:128], T.habs[:, 0:ALL].indirect(T.oz[:])).then_inc(S.szs, 1)
     sc.wait_ge(S.sya, 1)
+    sc.wait_ge(S.swr, 5)
     sc.wait_ge(S.soz, 1)
-    sc.activation(T.yb[:], T.ya[:, 0:272].indirect(T.oz[:]), F.Copy).then_inc(S.sy, 1)
-    done()
-    op(v.tensor_reduce(T.wa[:, 0:4], T.ght[:, :, 0, 0:16], X, A.add))
-    done()
-    v.transpose(T.wb[:], T.wa[:]).then_inc(S.swn, 1)
+    sc.activation(T.yb[:], T.ya[:, 0:ALL].indirect(T.oz[:]), F.Copy).then_inc(S.sy, 1)
+    sc.activation(T.wb[:], T.wr[:, 0:ALL].indirect(T.oz[:]), F.Copy).then_inc(S.swn, 1)
     sy.wait_ge(S.szq, 1)
     sy.dma_start(T.oc[:, 0:512], cod(T.zq, 0, 128)).then_inc(S.fin, 16)
     sy.wait_ge(S.sy, 1)
@@ -560,6 +568,6 @@ def rank_program(g, core, T, topo):
         q.wait_ge(S.szs, 1)
         q.dma_start(T.osc[4 * k:4 * k + 4, 0:128], T.zs[32 * k:32 * k + 4, 0:128]).then_inc(S.fin, 16)
     sy.wait_ge(S.swn, 1)
-    sy.dma_start(T.wn[0:1, 0:128], T.wb[0:4, 0:32]).then_inc(S.fin, 16)
+    sy.dma_start(T.wn[0:1, 0:128], T.wb[N:N + 1, 0:128]).then_inc(S.fin, 16)
     sy.wait_ge(S.fin, 112)
     g.wait_ge(S.loc, nl[0])

from concourse.bass import DstId, RemoteDMATransfer
from concourse.mybir import dt, AluOpType as A, AxisListType, ActivationFunctionType as F

C8, PL, BF, FP, I32, U16 = "float8_e4m3fn_x4", "uint8", "bfloat16", "float32", "int32", "uint16"
CAPP, CAPR, TOK, ZC = 48, 32, 128, 16
BIG, TINY, LOST, MID = 2.0 ** 98, 2.0 ** -120, 4096.0, 256
PLACES = 2 * TOK
OUT = 2 * TOK
ALL = ZC + 2 * TOK + OUT
SHAPES = {
    C8: "xq144 rq128 rn128 rp256 wq512 uq128 up128 vq128 xg384 he128 xe144 hx192 lx288 hp128 hq320 ho128 hr96 hb480 hab528 zq128",
    PL: "xs144 rs128 rns128 rps256 ws512 us128 ups128 vs128 xgs384 hes128 xes144 hxs192 lxs288 hpp128 hqs320 hos128 hps48 hrs192 hbs480 habs528 zs128",
    BF: "xt576 rtt704 wt2048 vt512 hto512 ht1152 vals32 win1280 nn128 nt128 on128 cs128 ct32 ot768 ge128 ww128 cc128 wr528",
    FP: "yb128 ya528 wb128 ff4 sb3 e_4 q_32 kb8 ka8 en8 c2_8 c3_8 dj64 thr64 cnt8 un8 ub8 nu8 sd8 ta24 tb24 qb128",
    I32: "ip1 ii4",
    U16: "lp8 lo8 of2 od24 oh16 oz8 le4",
}


def _split(s):
    k = len(s.rstrip("0123456789"))
    return s[:k], int(s[k:])


SCRATCH = {
    "gt": ("sbuf", [128, 8, 8], BF), "oh2": ("sbuf", [128, 2, 8], FP), "mk": ("sbuf", [128, 2, 8], FP),
    "pr": ("sbuf", [128, 2, 8], FP), "ph": ("sbuf", [128, 5, 8], FP), "dd": ("sbuf", [128, 12, 2, 16, 2], BF),
    "zst": ("sbuf", [128, 2, 32], FP), "zt": ("sbuf", [128, 2, 32], FP), "rz": ("sbuf", [128, 2, 128], BF),
    "d2": ("sbuf", [128, 8, 2, 16], BF), "dt": ("sbuf", [128, 8, 32], BF), "jw": ("sbuf", [128, 8, 8], FP), "j0": ("sbuf", [128, 8, 8], FP),
    "vv": ("sbuf", [128, 8, 2, 16], BF), "vvt": ("sbuf", [128, 8, 32], BF),
    "lv": ("sbuf", [128, 8, 2, 16], BF), "lvt": ("sbuf", [128, 8, 32], BF), "wp": ("sbuf", [128, 8, 8], FP),
    "ppt": ("sbuf", [128, 8, 8], FP), "vz": ("sbuf", [128, 8, 9], FP),
    "psa": ("psum", [128, 2048], FP), "psb": ("psum", [128, 2048], FP),
}
for _t, _s in SHAPES.items():
    for _w in _s.split():
        SCRATCH[_split(_w)[0]] = ("sbuf", [128, _split(_w)[1]], _t)
SEMAPHORES = ("v f gi ge1 gq gth gk gh ga sff swz scn srt sng sx sx0 sw su0 sv0 srq srp srps srz0 sxq mS snn sdd sde sg0 sg1 sg1s sg2 sg2s loc he he1 he2 de dl sep seps hd hret dsp dcr rsp rcr "
              "suq sup sups swq sz so so1 sro r1s r2s q1 q2 q3 soh sba sbas sbb sbbs mqa mqb sww scc svv soz szq szs my sya sy swr swn fin svq srz srd sz2 sz3 gz sd2 sjw ssb "
              "m0 m1 m2 m3 m4 m5 m6 m7 m8 m9 m10 m11").split()


def rank_program(g, core, T, topo):
    S = T.sem
    ranks = list(T.cores)
    N = len(ranks)
    u8, u32, X = dt.uint8, dt.uint32, AxisListType.X

    def order(r):
        rot = [(r + k) % N for k in range(1, N)]
        far = [q for q in rot if not topo.may_write(ranks[r], ranks[q])]
        near = [q for q in rot if topo.may_write(ranks[r], ranks[q])]
        return far, near

    def pos(r, q):
        far, near = order(r)
        return (far + near + [r]).index(q)

    def origin_of(r):
        return [q for q in order(r)[1] if order(q)[1][-1] == r][0]

    def late_of(r):
        return [q for q in order(r)[1] if q != origin_of(r)]

    def place(r, q):
        return (order(r)[0] + late_of(r)).index(q)

    def handers(r):
        c = ranks[r]
        can = [h for h in topo.cores_of(c) if h != c and all(topo.may_write(h, ranks[q]) for q in order(r)[0])]
        can = sorted(can, key=lambda h: (topo.die(h) == topo.die(c), h))[:4]
        return can + [h for h in topo.cores_of(c) if h != c and topo.die(h) == topo.die(c) and h not in can][:1]

    def send(dst_core, es, sem, src, dst):
        rid, pid = topo.addr(dst_core, core)
        return RemoteDMATransfer(dst_ids=[DstId(rid=rid, pnc=pid)], dma_engine_mask=sum(1 << e for e in es), remote_sem=sem, src=src, dst=dst)

    def cod(t, a, b):
        return t[:, a:b].bitcast(u8)

    def run(planes, c, p, a, b):
        return p[:, a:b] if planes else cod(c, a, b)

    def w32(t, a, b):
        return t[:, a:b].bitcast(u32)

    def share(es, k):
        m = len(es) // k
        return [es[m * i:m * i + m] for i in range(k)]

    def off(r):
        return topo.engines(ranks[r], ranks[order(r)[1][0]])

    def inside(r, k):
        es = topo.engines(ranks[r], handers(r)[k])
        return [e for e in es if e not in off(r)] if k == 4 else es if k < 2 else share(es, 2)[k % 2]

    def ahead(r, k):
        return inside(r, k) if k == 4 else share(topo.engines(ranks[r], handers(r)[k]), 4)[k]

    rank = T.rank_of(core)

    if rank is None:
        mine = [r for r in range(N) if ranks[r] in topo.cores_of(core)]
        if not mine or core not in handers(mine[0]):
            return
        r = mine[0]
        far, near = order(r)
        i = handers(r).index(core)
        n = [0]

        def hand(planes, sem_in, cnt, sem, bc, bp, dc, dp, jobs):
            g.wait_ge(sem_in, cnt)
            t = []
            for es, (q, a, b, m) in zip(share(topo.engines(core, ranks[jobs[0][0]]), len(jobs)), jobs):
                t.append(send(ranks[q], es, sem, run(planes, bc, bp, a, a + m), run(planes, dc, dp, b, b + m)))
                n[0] += len(es)
            g.remote_dma_fused(t, local_sem=S.loc)
        m, cnt = TOK // 4, len(inside(r, i))
        hand(i == 4, S.he, len(ahead(r, i)), S.de, T.he, T.hes, T.xe, T.xes, [(near[-1], 0, ZC, TOK) if i == 4 else (near[-1], 0, ZC + m * i, m)])
        to, out, s_out = (near[:2], CAPP, S.dsp) if i == 4 else (far[2 * (i % 2):2 * (i % 2) + 2], 0, S.dcr)
        hand(i >= 2, S.hd, cnt, s_out, T.hx, T.hxs, T.lx, T.lxs, [(q, out + CAPP * k, CAPP * place(q, r), CAPP) for k, q in enumerate(to)])
        if i == 4:
            q = origin_of(r)
            for planes, sem in ((False, S.he1), (True, S.he2)):
                hand(planes, sem, cnt, S.rsp, T.hr, T.hps, T.hb, T.hbs, [(q, 0, ZC + CAPP * pos(q, r), CAPP)])
            q = late_of(r)[1]
            hand(True, S.hret, cnt, S.rsp, T.hr, T.hrs, T.hb, T.hbs, [(q, 3 * CAPP, ZC + CAPP * pos(q, r), CAPP)])
        else:
            hand(i >= 2, S.hret, cnt, S.rcr, T.hr, T.hrs, T.hb, T.hbs, [(q, CAPP * k, ZC + CAPP * pos(q, r), CAPP) for k, q in enumerate(to)])
        g.wait_ge(S.loc, n[0])
        return

    far, near = order(rank)
    lists = far + near[:2] + [rank] + near[2:]
    half, own, rest = CAPP * len(far), CAPP * (N - 1), CAPP * len(near)
    origin, late, fifth = origin_of(rank), late_of(rank), handers(rank)[4]
    two = 2 * CAPP
    over = 128 - two
    eng = len(off(rank))
    ahead_in = sum(len(topo.engines(h, core)) for h in handers(origin))
    near_in, near_back = 2 * eng, 5 * eng
    far_in = sum(2 * len(share(topo.engines(handers(q)[0], core), 2)[0]) for q in far)
    v, sc, te, sy = g.vector, g.scalar, g.tensor, g.sync
    n, nf, nl = [0], [0], [0]

    def op(c):
        c.then_inc(S.v, 1)
        n[0] += 1

    def done():
        v.wait_ge(S.v, n[0])

    def fl(c):
        c.then_inc(S.f, 1)
        nf[0] += 1

    def fdone():
        v.wait_ge(S.f, nf[0])

    def tt(*a):
        op(v.tensor_tensor(*a))

    def ts(*a):
        op(v.tensor_scalar(*a))

    def fused(t, *waits):
        for s, k in waits:
            g.wait_ge(s, k)
        g.remote_dma_fused([send(*a) for a in t], local_sem=S.loc)
        nl[0] += sum(len(a[1]) for a in t)

    def to_far(parts, wait, sem, dc, dp):
        for i, (bc, bp, a, s) in enumerate(parts):
            fused([(handers(rank)[i], inside(rank, i), sem, cod(bc, a, a + two), cod(dc, 0, two))], (s, 1))
        fused([(handers(rank)[2 + i], inside(rank, 2 + i), sem, bp[:, a:a + two], dp[:, 0:two]) for i, (bc, bp, a, s) in enumerate(parts)], wait)

    def to_near(to, first, bc, dc, sem):
        t = []
        for i, (q, b) in enumerate(to):
            a = first + CAPP * i
            t.append((ranks[q], share(off(rank), len(to))[i], sem, cod(bc, a, a + CAPP), cod(dc, b, b + CAPP)))
        return t

    def zeros(m):
        return T.rtt[:, 32:32 + m]

    sc.dma_start(T.rtt[:, 0:32], T.rt[:, 0:32]).then_inc(S.srt, 16)
    sy.dma_start(T.xt[:, 4 * ZC:4 * ZC + 512], T.x[:]).then_inc(S.sx, 16)
    sy.dma_start(T.wt[:], T.w[:]).then_inc(S.sw, 16)
    sy.dma_start(T.rtt[:, 576:704], T.u[:, 0:128]).then_inc(S.su0, 16)

    def iota(out, pattern, base, sem):
        g.iota(out, pattern, base, 0, allow_small_or_imprecise_dtypes=True).then_inc(sem, 1)

    def columns(out, value, sem):
        i, k = 0, 0
        while i < N:
            m = 1
            while i + m < N and lists[i + m] == lists[i] + 2 * m and (m == 1 or value(lists[i + m]) - value(lists[i + m - 1]) == value(lists[i + 1]) - value(lists[i])):
                m += 1
            a, step = lists[i], value(lists[i + 1]) - value(lists[i]) if m > 1 else 0
            iota(out[:, a:a + 2 * m - 1:2], [[step, m]], value(a), sem)
            i, k = i + m, k + 1
        return k

    def first(e):
        i = lists.index(e)
        return PLACES * (i // 4 * 2 + i % 2 + 1) + i % 4 // 2
    g.iota(T.ip[:], [[0, 1]], 0, 1).then_inc(S.gi, 1)
    iota(T.e_[:], [[2, 4]], 32 - N, S.ge1)
    iota(T.dj[:], [[1, N], [-1, N]], 0, S.gth)
    iota(T.q_[:], [[0, 2], [1, 16]], ZC, S.gq)
    nk = columns(T.kb, lambda e: first(e) - 2, S.gk)

    m = TOK // 4
    fused([(handers(rank)[k], ahead(rank, k), S.he, cod(T.xq, ZC + m * k, ZC + m * k + m), cod(T.he, 0, m)) for k in range(4)], (S.sxq, 1))
    fused([(fifth, ahead(rank, 4), S.he, T.xs[:, ZC:ZC + TOK], T.hes[:, 0:TOK])])
    na = columns(T.ka, lambda e: 2 * (ZC + CAPP * pos(rank, e) + over * (e == rank) - 1), S.ga)
    iota(T.en[:], [[1, N]], 0, S.ga)
    na += 1
    iota(T.zst[:, :, N + 1:32], [[0, 2], [0, 31 - N]], 0, S.gz)

    op(v.memset(zeros(512), 0.0))
    v.wait_ge(S.gi, 1)
    ts(T.ii[:, 0:1], T.ip[:], 7, None, A.bitwise_and)
    ts(T.ii[:, 1:2], T.ip[:], 3, 1, A.logical_shift_right, A.bitwise_and)
    fl(v.tensor_scalar(T.ii[:, 2:3], T.ip[:], 112, None, A.bitwise_and))
    fl(v.tensor_scalar(T.ii[:, 3:4], T.ip[:], 15, None, A.bitwise_and))
    done()
    op(v.tensor_copy(T.ff[:, 0:2], T.ii[:, 0:2]))
    v.quantize_mx(T.rp[:, 128:256], T.rps[:, 128:256], zeros(512)).then_inc(S.srz0, 1)
    v.wait_ge(S.ge1, 1)
    done()
    op(v.tensor_scalar(T.lp[:, 0:4], T.e_[:], 0.0, T.ff[:, 0:1], A.mult, A.add))
    op(v.tensor_scalar(T.lp[:, 4:8], T.e_[:], T.ff[:, 1:2], None, A.add))
    listed_pairs = n[0]
    fdone()
    v.tensor_copy(T.ff[:, 2:4], T.ii[:, 2:4]).then_inc(S.sff, 1)
    v.wait_ge(S.gth, 1)
    fl(v.tensor_scalar(T.thr[:], T.dj[:], 0.0, TINY, A.is_le, A.mult))

    sc.wait_ge(S.v, 1)
    sc.activation(T.xt[:, 0:4 * ZC], zeros(4 * ZC), F.Copy).then_inc(S.sx0, 1)
    sc.activation(T.on[:], zeros(128), F.Copy).then_inc(S.sx0, 1)
    for k in range(1, 5):
        sc.activation(T.win[:, PLACES * k:PLACES * k + two], zeros(two), F.Copy).then_inc(S.swz, 1)
    sc.wait_ge(S.sx0, 2)
    sc.activation(T.on[64:96, 32:64], T.rtt[64:96, 32:64], F.Copy, bias=1.0).then_inc(S.swz, 1)
    sc.activation(T.on[96:128, 32:96], T.rtt[96:128, 32:96], F.Copy, bias=1.0).then_inc(S.swz, 1)

    sc.wait_ge(S.srt, 16)
    sc.activation(T.rtt[:, 544:576], T.rtt[:, 0:32], F.Copy, scale=-1.0).then_inc(S.sng, 1)
    v.wait_ge(S.srt, 16)
    done()
    v.quantize_mx(T.rq[:], T.rs[:], T.rtt[:, 0:512]).then_inc(S.srq, 1)
    v.wait_ge(S.sng, 1)
    v.quantize_mx(T.rn[:], T.rns[:], T.rtt[:, 64:576]).then_inc(S.srq, 1)
    sc.wait_ge(S.v, listed_pairs)
    for k, (q_, s_, a) in enumerate(((T.rq, T.rs, 0), (T.rn, T.rns, 96))):
        b = 64 - 64 * k
        if k:
            v.wait_ge(S.sx0, 2)
            v.wait_ge(S.sx, 16)
            v.quantize_mx(T.xq[:], T.xs[:], T.xt[:]).then_inc(S.sxq, 1)
        v.wait_ge(S.srq, k + 1)
        v.tensor_copy(w32(T.rp, b, b + 64), w32(q_, a, 128).indirect(T.lp[:, 4 * k:4 * k + 4])).then_inc(S.srp, 1)
        sc.wait_ge(S.srq, k + 1)
        sc.activation(T.rps[:, b:b + 64], s_[:, a:128].indirect(T.lp[:, 4 * k:4 * k + 4]), F.Copy).then_inc(S.srps, 1)
    sc.wait_ge(S.sff, 1)
    sc.wait_ge(S.gq, 1)
    sc.activation(T.sb[:, 2:3], T.ff[:, 3:4], F.Sign, bias=-N - 0.5).then_inc(S.ssb, 1)
    sc.activation(T.vals[:], T.q_[:], F.Identity, bias=T.ff[:, 2:3]).then_inc(S.scn, 1)
    te.wait_ge(S.srz0, 1)
    te.wait_ge(S.sxq, 1)
    for k in range(2):
        b = 64 - 64 * k
        te.wait_ge(S.srp, k + 1)
        te.wait_ge(S.srps, k + 1)
        c = te.matmul_mx(T.psb[:, 0:128], T.xq[:, ZC:ZC + TOK], T.xs[:, ZC:ZC + TOK], T.rp[:, b:b + 128], T.rps[:, b:b + 128], k == 0, k == 1)
    c.then_inc(S.mS, 1)
    fl(v.memset(T.nn[:], 0.0))
    fl(v.memset(T.lo[:], 0))

    v.wait_ge(S.mS, 1)
    fdone()
    tt(T.gt[:], T.psb[:, 0:64], T.thr[:], A.is_ge)
    done()
    op(v.tensor_reduce(T.cnt[:], T.gt[:], X, A.add))
    counted = n[0]
    done()
    for d, b, p, c in ((64, 0, 64, 0), (32, 0, 32, 0), (0, 0, 128, 96)):
        ts(T.nn[d:d + p, c:c + 8], T.cnt[b:b + p, :], 1.5, 2.0, A.is_le, A.mult)
    sc.wait_ge(S.v, counted)
    sc.wait_ge(S.f, nf[0])
    for d, b, p, c in ((64, 32, 32, 32), (96, 0, 32, 32), (96, 64, 32, 64)):
        sc.activation(T.nn[d:d + p, c:c + 8], T.cnt[b:b + p, :], F.Sign, scale=-1.0, bias=1.5).then_inc(S.snn, 1)
    sc.wait_ge(S.ssb, 1)
    sc.activation(T.sb[:, 0:1], T.sb[:, 2:3], F.Copy, scale=-0.25, bias=0.75).then_inc(S.ssb, 1)
    sc.activation(T.sb[:, 1:2], T.sb[:, 2:3], F.Copy, scale=-0.5 * MID, bias=-0.5 * MID).then_inc(S.ssb, 1)
    fl(v.tensor_scalar(T.oh2[:, 0, :], T.cnt[:], 0.0, None, A.is_equal))
    v.wait_ge(S.snn, 3)
    done()
    op(v.transpose(T.nt[:], T.nn[:]))
    fl(v.tensor_scalar(T.oh2[:, 1, :], T.cnt[:], 1.0, None, A.is_equal))
    v.wait_ge(S.swz, 6)
    done()
    op(v.tensor_tensor_scan(T.cs[:], T.nt[:], T.on[:], 0.0, A.add, A.add))
    v.wait_ge(S.f, nf[0] - 1)
    v.wait_ge(S.gk, nk)
    fl(v.tensor_tensor(T.mk[:, 0, :], T.oh2[:, 0, :], T.kb[:], A.mult))
    done()
    op(v.transpose(T.ct[:], T.cs[:, 96:128]))
    v.wait_ge(S.f, nf[0] - 1)
    fl(v.tensor_tensor(T.mk[:, 1, :], T.oh2[:, 1, :], T.kb[:], A.mult))
    done()
    tt(T.pr[:, 0, :], T.mk[:, 0, :], T.ct[:, 0:8], A.add)
    fdone()
    tt(T.pr[:, 1, :], T.mk[:, 1, :], T.ct[:, 0:8], A.add)
    fl(v.tensor_tensor(T.sd[:], T.oh2[:, 1, :], T.oh2[:, 0, :], A.subtract))
    done()
    op(v.tensor_reduce(T.of[:], T.pr[:], X, A.max))
    fl(v.tensor_scalar(T.nu[:], T.ct[:, 0:8], 2.0 * CAPP, 2.0, A.is_gt, A.mult))
    v.wait_ge(S.scn, 1)
    done()
    op(v.tensor_copy(T.win[:].indirect(T.of[:]), T.vals[:]))
    scattered = n[0]
    fl(v.tensor_scalar(T.un[:], T.ct[:, 0:8], 2.0 * CAPP, None, A.is_le))
    done()

    def lay(k, d):
        return T.dd[:, 3 * k:3 * k + 3, d, :, :], T.win[:, PLACES * (k + 1):PLACES * (k + 1) + two]

    def turn(h, j):
        return v.transpose(T.ot[:, 384 * h + 192 * j:384 * h + 192 * j + 192], T.dd[:, 6 * h:6 * h + 6, :, :, j])
    sc.wait_ge(S.v, scattered)
    sc.activation(*lay(0, 1), F.Copy).then_inc(S.sdd, 1)
    for k, d in ((2, 0), (2, 1), (3, 0)):
        sc.activation(*lay(k, d), F.Copy).then_inc(S.sde, 1)
    for k, d in ((0, 0), (1, 0), (1, 1)):
        op(v.tensor_copy(*lay(k, d)))
    fl(v.tensor_scalar(T.ub[:], T.ct[:, 0:8], 2.0 * CAPP, BIG, A.is_le, A.mult))
    v.wait_ge(S.sdd, 1)
    done()
    op(turn(0, 0))
    op(turn(0, 1))
    fl(v.tensor_copy(*lay(3, 1)))
    done()
    tt(T.ta[:, 0:12], T.ot[:, 0:384:32], T.ot[:, 16:384:32], A.add)
    v.wait_ge(S.sde, 3)
    fdone()
    fl(turn(1, 0))
    done()
    tt(T.tb[0:64, 0:12], T.ta[0:64, 0:12], T.ta[64:128, 0:12], A.add)
    fl(turn(1, 1))
    done()
    for p in (0, 32, 64, 96):
        tt(T.od[p:p + 32, 0:12], T.tb[0:32, 0:12], T.tb[32:64, 0:12], A.add)
    far_list = n[0]
    fdone()
    fl(v.tensor_tensor(T.ta[:, 12:24], T.ot[:, 384:768:32], T.ot[:, 400:768:32], A.add))

    def picked(lo, hi, s1, s2):
        a, b = 16 * lo, 16 * hi
        v.tensor_copy(w32(T.xg, a, b), w32(T.xq, 0, ZC + TOK).indirect(T.od[:, lo:hi])).then_inc(s1, 1)
        sc.activation(T.xgs[:, a:b], T.xs[:, 0:ZC + TOK].indirect(T.od[:, lo:hi]), F.Copy).then_inc(s2, 1)
    done()
    sc.wait_ge(S.sxq, 1)
    sc.wait_ge(S.v, far_list)
    picked(0, 6, S.sg0, S.sg1s)
    picked(6, 12, S.sg1, S.sg1s)
    fdone()
    tt(T.tb[0:64, 12:24], T.ta[0:64, 12:24], T.ta[64:128, 12:24], A.add)
    done()
    for p in (0, 32, 64, 96):
        tt(T.od[p:p + 32, 12:24], T.tb[0:32, 12:24], T.tb[32:64, 12:24], A.add)
    near_list = n[0]
    v.wait_ge(S.ga, na)
    fl(v.tensor_tensor(T.c3_[:], T.ct[:, 0:8], T.ka[:], A.add))
    done()
    sc.activation(T.xes[:, 0:ZC], T.xs[:, 0:ZC + TOK].indirect(T.lo[:, 0:1]), F.Copy).then_inc(S.sz, 1)
    sc.wait_ge(S.v, near_list)
    picked(12, 21, S.sg2, S.sg2s)
    fdone()
    fl(v.tensor_tensor(T.c2_[:], T.un[:], T.c3_[:], A.mult))
    fl(v.tensor_copy(w32(T.xe, 0, ZC), w32(T.xq, 0, ZC + TOK).indirect(T.lo[:, 0:1])))

    to_far([(T.xg, T.xgs, 0, S.sg0), (T.xg, T.xgs, two, S.sg1)], (S.sg1s, 2), S.hd, T.hx, T.hxs)
    fused([(ranks[near[2]], off(rank), S.dl, T.od[:, 21:24], T.le[:, 0:3])], (S.v, near_list))
    fused(to_near([(q, CAPP * place(q, rank)) for q in near[:2]], half, T.xg, T.lx, S.dsp)
          + [(fifth, inside(rank, 4), S.hd, T.xgs[:, half - CAPP:half + 3 * CAPP], T.hxs[:, 0:4 * CAPP])], (S.sg2, 1), (S.sg2s, 1))
    iota(T.j0[:], [[16, 8], [0, 8]], ZC, S.gh)
    iota(T.vz[:, :, N:N + 1], [[0, 8]], 0, S.gh)
    iota(T.wr[:, 0:ZC], [[0, ZC]], -100, S.gh)

    v.wait_ge(S.sw, 16)
    for i in range(4):
        v.quantize_mx(T.wq[:, 128 * i:128 * i + 128], T.ws[:, 128 * i:128 * i + 128], T.wt[:, 512 * i:512 * i + 512]).then_inc(S.swq, 1)
    sy.wait_ge(S.swq, 4)
    sy.dma_start(T.vt[:], T.v[:]).then_inc(S.sv0, 16)

    a = half + rest
    fdone()
    sc.wait_ge(S.sz, 1)
    for q in (v, sc):
        q.wait_ge(S.de, ahead_in)
        q.wait_ge(S.dl, eng)
    v.tensor_copy(w32(T.xg, a, a + CAPP), w32(T.xe, 0, ZC + TOK).indirect(T.le[:, 0:3])).then_inc(S.sep, 1)
    sc.activation(T.xgs[:, a:a + CAPP], T.xes[:, 0:ZC + TOK].indirect(T.le[:, 0:3]), F.Copy).then_inc(S.seps, 1)

    tt(T.ph[:, 3, :], T.sd[:], T.ub[:], A.mult)
    tt(T.ph[:, 4, :], T.oh2[:, 0, :], T.en[:], A.mult)
    termed = n[0]
    tt(T.ph[:, 0, :], T.oh2[:, 1, :], T.en[:], A.mult)
    for k in range(2):
        tt(T.ph[:, 1 + k, :], T.oh2[:, k, :], T.c2_[:], A.mult)
    v.wait_ge(S.v, termed)
    fl(v.tensor_reduce(T.zst[:, 1, N - 1:N + 1], T.ph[:, 3:5, :], X, A.add))
    tt(T.zst[:, 0, 0:N], T.cnt[:], T.nu[:], A.add)
    v.wait_ge(S.gz, 1)
    v.wait_ge(S.v, n[0] - 1)
    op(v.tensor_reduce(T.zst[:, 0, N:N + 3], T.ph[:, 0:3, :], X, A.add))
    fdone()
    ts(T.zst[:, 1, 0:N - 1], zeros(N - 1), T.zst[:, 1, N - 1:N], None, A.add)

    def expert(h, waits, ps, xc, xp, a, m, skip, tile, t0, vecs, rs, outs):
        for s, k in waits:
            te.wait_ge(s, k)
        for i in range(4):
            te.matmul_mx(ps[:, 512 * i:512 * i + m], T.wq[:, 128 * i:128 * i + 128], T.ws[:, 128 * i:128 * i + 128],
                         xc[:, a:a + m], xp[:, a:a + m], True, True).then_inc(S["m%d" % (4 * h + i)], 1)
        for i in range(4):
            src, dst = ps[:, 512 * i + skip:512 * i + m], tile[:, 4 * (t0 + skip) + i:4 * (t0 + m):4]
            q = v if i in vecs else sc
            q.wait_ge(S["m%d" % (4 * h + i)], 1)
            if i in vecs:
                ts(dst, src, 0.0, 0.0625, A.max, A.mult)
            else:
                sc.activation(dst, src, F.Relu, scale=0.0625).then_inc(rs, 1)
        v.wait_ge(rs, 4 - len(vecs))
        done()
        for oc, os_, b, sem in outs:
            v.quantize_mx(oc, os_, tile[:, 4 * b:4 * b + 512]).then_inc(sem, 1)

    expert(2, ((S.sg2, 1), (S.sg2s, 1), (S.swq, 4), (S.sep, 1), (S.seps, 1)), T.psa, T.xg, T.xgs, a + CAPP - 128, 128, 0, T.hto, 0,
           (3,), S.sro, [(T.ho[:], T.hos[:], 0, S.so1)])
    op(v.transpose(T.zt[:], T.zst[:]))
    turned = n[0]
    a = 128 - CAPP
    fused([(fifth, inside(rank, 4), S.he1, cod(T.ho, a, 128), cod(T.hr, 0, CAPP))], (S.so1, 1))
    fused([(fifth, inside(rank, 4), S.he2, T.hos[:, a:128], T.hps[:, 0:CAPP])])
    a = half - 128
    expert(1, ((S.dcr, far_in),), T.psb, T.lx, T.lxs, 0, half, 0, T.ht, 0, (1, 3), S.r2s,
           [(T.hp[:], T.hpp[:], 0, S.q3), (T.hq[:, a:half], T.hqs[:, a:half], a, S.q2)])
    to_far([(T.hp, T.hpp, 0, S.q3), (T.hq, T.hqs, two, S.q2)], (S.q2, 1), S.hret, T.hr, T.hrs)
    expert(0, ((S.so1, 1), (S.dsp, near_in)), T.psa, T.lx, T.lxs, half - over, 128, over, T.ht, half - over, (3,), S.r1s,
           [(T.hq[:, half:half + 128], T.hqs[:, half:half + 128], half - over, S.q1)])
    back = [(q, ZC + CAPP * pos(q, rank)) for q in late]
    a, b = half + over, back[0][1]
    fused(to_near(back, a, T.hq, T.hb, S.rsp) + [(fifth, inside(rank, 4), S.hret, T.hqs[:, a - two:a + two], T.hrs[:, 0:4 * CAPP])], (S.q1, 1))
    fused([(ranks[late[0]], off(rank), S.rsp, T.hqs[:, a:a + CAPP], T.hbs[:, b:b + CAPP])])

    sc.wait_ge(S.v, turned)
    sc.wait_ge(S.ssb, 3)
    for b in range(4):
        sc.activation(T.rz[0:32, :, 32 * b:32 * b + 32], T.zt[32 * b:32 * b + 32, :, :], F.Identity, scale=T.sb[0:32, 0:1], bias=T.sb[0:32, 1:2]).then_inc(S.srz, 1)
    v.wait_ge(S.srz, 4)
    op(v.tensor_copy(T.rz[32:64], T.rz[0:32]))
    v.quantize_mx(T.hb[:, ZC + own:ZC + own + 128], T.hbs[:, ZC + own:ZC + own + 128], T.hto[:]).then_inc(S.so, 1)
    done()
    v.tensor_copy(T.rz[64:128], T.rz[0:64]).then_inc(S.srd, 1)
    v.wait_ge(S.su0, 16)
    v.quantize_mx(T.uq[:], T.us[:], T.rtt[:, 192:704]).then_inc(S.suq, 1)
    for q_, s_ in ((T.hb, T.hbs), (T.hab, T.habs)):
        op(v.tensor_copy(w32(q_, 0, ZC), w32(T.xq, 0, ZC + TOK).indirect(T.lo[:, 0:1])))
        sc.activation(s_[:, 0:ZC], T.xs[:, 0:ZC + TOK].indirect(T.lo[:, 0:1]), F.Copy).then_inc(S.sz2, 1)
    v.wait_ge(S.suq, 1)
    v.tensor_copy(w32(T.up, 0, 128), w32(T.uq, 96, 128).indirect(T.lo[:])).then_inc(S.sup, 1)
    sc.wait_ge(S.gh, 3)
    sc.activation(T.jw[:], T.j0[:], F.Identity, bias=T.ff[:, 3:4]).then_inc(S.sjw, 1)
    sc.wait_ge(S.srd, 1)
    for d in range(2):
        sc.activation(T.d2[:, :, d, :], T.rz[:, 0, :], F.Copy).then_inc(S.sd2, 1)
    sc.wait_ge(S.suq, 1)
    sc.activation(T.ups[:, 0:128], T.us[:, 96:128].indirect(T.lo[:]), F.Copy).then_inc(S.sups, 1)
    v.wait_ge(S.sd2, 2)
    op(v.transpose(T.dt[:], T.d2[:]))
    v.wait_ge(S.sv0, 16)
    v.quantize_mx(T.vq[:], T.vs[:], T.vt[:]).then_inc(S.svq, 1)
    done()
    ts(T.wp[:], T.dt[:, :, 0:N], 1.0 * TOK, None, A.mult)
    for k in range(2):
        v.tensor_scalar(T.oh[:, 8 * k:8 * k + 8], T.dt[:, :, N + 1 + k], 1.0 * MID, None, A.add).then_inc(S.soh, 1)
    v.wait_ge(S.sjw, 1)
    v.wait_ge(S.gh, 3)
    done()
    tt(T.ppt[:], T.wp[:], T.jw[:], A.add)
    for a in range(ZC + 2 * TOK, ALL, 128):
        v.quantize_mx(T.hab[:, a:a + 128], T.habs[:, a:a + 128], zeros(512)).then_inc(S.sz3, 1)
    sc.activation(T.ya[:, ZC + 2 * TOK:ALL], zeros(OUT), F.Copy).then_inc(S.swr, 1)
    for k in range(2):
        a = ZC + TOK * k
        sc.activation(T.wr[:, a:a + TOK], T.rz[:, 1 - k, :], F.Copy).then_inc(S.swr, 1)
        sc.activation(T.wr[:, a + OUT:a + OUT + TOK], T.rz[:, 1 - k, :], F.Copy, scale=-1.0, bias=-1.0).then_inc(S.swr, 1)
    done()

    for q in (v, sc):
        q.wait_ge(S.soh, 2)
        q.wait_ge(S.so, 1)
        q.wait_ge(S.sz3, 2)
        q.wait_ge(S.rsp, near_back)
        q.wait_ge(S.rcr, far_in)
    sc.wait_ge(S.sz2, 2)
    for k, s1, s2 in ((1, S.sbb, S.sbbs), (0, S.sba, S.sbas)):
        a = ZC + TOK * k
        v.tensor_copy(w32(T.hab, a, a + 128), w32(T.hb, 0, 480).indirect(T.oh[:, 8 * k:8 * k + 8])).then_inc(s1, 1)
        sc.activation(T.habs[:, a:a + 128], T.hbs[:, 0:480].indirect(T.oh[:, 8 * k:8 * k + 8]), F.Copy).then_inc(s2, 1)
    for s in (S.sup, S.sups, S.svq, S.sbb, S.sbbs):
        te.wait_ge(s, 1)
    te.matmul_mx(T.psa[:, 0:128], T.up[:, 0:128], T.ups[:, 0:128], T.hab[:, ZC + TOK:ZC + 2 * TOK], T.habs[:, ZC + TOK:ZC + 2 * TOK], True, True).then_inc(S.mqb, 1)
    te.wait_ge(S.sba, 1)
    te.wait_ge(S.sbas, 1)
    te.matmul_mx(T.psa[:, 512:640], T.up[:, 0:128], T.ups[:, 0:128], T.hab[:, ZC:ZC + TOK], T.habs[:, ZC:ZC + TOK], True, True).then_inc(S.mqa, 1)
    te.matmul_mx(T.psa[:, 1024:1296], T.vq[:, 0:128], T.vs[:, 0:128], T.hab[:, 0:272], T.habs[:, 0:272], True, True).then_inc(S.my, 1)
    v.wait_ge(S.mqb, 1)
    tt(T.qb[:], T.psa[:, 0:128], T.rz[:, 1, :], A.add)
    v.wait_ge(S.mqa, 1)
    done()
    tt(T.ge[:], T.psa[:, 512:640], T.qb[:], A.is_lt)
    done()
    v.tensor_tensor(T.ww[:], T.ge[:], T.rz[:, 0, :], A.is_equal).then_inc(S.sww, 1)
    v.wait_ge(S.sww, 1)
    v.tensor_tensor_scan(T.cc[:], T.ww[:], T.ww[:], 0.0, A.add, A.max).then_inc(S.scc, 1)
    fl(v.tensor_scalar(T.vv[:, :, 0, :], T.ww[:], 1.0, LOST, A.subtract, A.mult))
    sc.wait_ge(S.my, 1)
    sc.activation(T.ya[:, 0:ZC + 2 * TOK], T.psa[:, 1024:1296], F.Copy).then_inc(S.sya, 1)
    sc.wait_ge(S.sww, 1)
    sc.activation(T.vv[:, :, 1, :], T.ww[:], F.Copy, scale=LOST, bias=-LOST).then_inc(S.svv, 1)
    v.wait_ge(S.scc, 1)
    for d in range(2):
        ts(T.lv[:, :, d, :], T.cc[:], 1.0 * CAPR, 1.0 * OUT, A.is_gt, A.mult)
    fdone()
    v.wait_ge(S.svv, 1)
    fl(v.transpose(T.vvt[:], T.vv[:]))
    done()
    op(v.transpose(T.lvt[:], T.lv[:]))
    fdone()
    fl(v.tensor_tensor(T.wp[:], T.vvt[:, :, 0:8], T.ppt[:], A.add))
    fdone()
    done()
    tt(T.vz[:, :, 0:8], T.wp[:], T.lvt[:, :, 0:8], A.add)
    done()
    v.tensor_reduce(T.oz[:], T.vz[:], X, A.max).then_inc(S.soz, 1)
    v.wait_ge(S.soz, 1)
    v.tensor_copy(w32(T.zq, 0, 128), w32(T.hab, 0, ALL).indirect(T.oz[:])).then_inc(S.szq, 1)
    v.tensor_copy(T.zs[:, 0:128], T.habs[:, 0:ALL].indirect(T.oz[:])).then_inc(S.szs, 1)
    sc.wait_ge(S.sya, 1)
    sc.wait_ge(S.swr, 5)
    sc.wait_ge(S.soz, 1)
    sc.activation(T.yb[:], T.ya[:, 0:ALL].indirect(T.oz[:]), F.Copy).then_inc(S.sy, 1)
    sc.activation(T.wb[:], T.wr[:, 0:ALL].indirect(T.oz[:]), F.Copy).then_inc(S.swn, 1)
    sy.wait_ge(S.szq, 1)
    sy.dma_start(T.oc[:, 0:512], cod(T.zq, 0, 128)).then_inc(S.fin, 16)
    sy.wait_ge(S.sy, 1)
    sy.dma_start(T.y[:], T.yb[:]).then_inc(S.fin, 16)
    for k in range(4):
        q = sc if k % 2 else sy
        q.wait_ge(S.szs, 1)
        q.dma_start(T.osc[4 * k:4 * k + 4, 0:128], T.zs[32 * k:32 * k + 4, 0:128]).then_inc(S.fin, 16)
    sy.wait_ge(S.swn, 1)
    sy.dma_start(T.wn[0:1, 0:128], T.wb[N:N + 1, 0:128]).then_inc(S.fin, 16)
    sy.wait_ge(S.fin, 112)
    g.wait_ge(S.loc, nl[0])
